import numpy as np
import ml_dtypes


def mxq(x, axis, fmt="e4m3"):
    dtype, down = {"e4m3": (ml_dtypes.float8_e4m3fn, 7), "e5m2": (ml_dtypes.float8_e5m2, 14)}[fmt]
    v = np.moveaxis(np.asarray(x, np.float32).astype(ml_dtypes.bfloat16).astype(np.float64), axis, -1)
    blocks = v.reshape(v.shape[:-1] + (-1, 32))
    amax = np.abs(blocks).max(-1, keepdims=True)
    byte = np.maximum(np.where(amax > 0, np.frexp(amax)[1] - 1 + 127, 0) - down, 1)
    scale = np.exp2(byte - 127.0)
    codes = (blocks / scale).astype(np.float32).astype(dtype).astype(np.float64)
    return np.moveaxis((codes * scale).reshape(v.shape), -1, axis)


WIDE = False


def mx_kscale(k):
    if not WIDE:
        return np.ones(k)
    levels = np.array([10, -10, 5, -5, 0])
    if k % 512:
        return np.exp2(np.random.permutation(np.resize(levels, k // 32))).repeat(32)
    a = np.empty((k // 512, 16))
    for p in range(k // 512):
        a[p, :8] = np.random.permutation(np.resize(levels, 8))
        for g in range(8):
            far = levels[np.abs(levels - a[p, g]) >= 10]
            a[p, g + 8] = far[np.random.randint(len(far))]
    return np.exp2(a.ravel()).repeat(32)


BF16 = ml_dtypes.bfloat16


def bf(x):
    return np.asarray(x, np.float32).astype(BF16)


def f64(x):
    return np.asarray(x).astype(np.float64)


E2M1 = np.array([0.0, 0.5, 1.0, 1.5, 2.0, 3.0, 4.0, 6.0, -0.0, -0.5, -1.0, -1.5, -2.0, -3.0, -4.0, -6.0])


def pack_weight(w, fmt):
    k, n = w.shape
    w = f64(bf(w)).reshape(k // 32, 32, n)
    amax = np.abs(w).max(1)
    if fmt == "e4m3":
        byte = np.frexp(amax)[1] - 1 + 127 - 7
    else:
        mant, ex = np.frexp(amax / 6.0)
        byte = np.where(mant > 0.5, ex, ex - 1) + 127
    byte = np.clip(np.where(amax > 0, byte, 1), 1, 254)
    scaled = (w * np.exp2(127.0 - byte)[:, None, :]).reshape(k, n).astype(np.float32)
    by_word = np.ascontiguousarray(scaled.reshape(k // 512, 128, 4, n).transpose(0, 1, 3, 2))
    if fmt == "e4m3":
        words = by_word.astype(ml_dtypes.float8_e4m3fn).view(np.uint8)
    else:
        c = by_word.astype(ml_dtypes.float4_e2m1fn).view(np.uint8) & 0xF
        words = c[..., 0::2] | (c[..., 1::2] << 4)
    return np.ascontiguousarray(words), np.ascontiguousarray(byte.astype(np.uint8).reshape(k // 512, 16, n))


def unpack_weight(words, scales, fmt):
    g, p, n, _ = words.shape
    if fmt == "e4m3":
        vals = np.ascontiguousarray(words).view(ml_dtypes.float8_e4m3fn).astype(np.float64)
    else:
        nib = np.empty((g, p, n, 4), np.uint8)
        nib[..., 0::2] = words & 0xF
        nib[..., 1::2] = words >> 4
        vals = E2M1[nib]
    vals = vals * np.repeat(np.exp2(scales.astype(np.float64) - 127.0), 8, axis=1)[..., None]
    return vals.transpose(0, 1, 3, 2).reshape(g * 512, n)
def pack4(w):
    words, scales = pack_weight(w, "e2m1")
    return words.reshape(words.shape[0], 128, -1), scales


def unpack4(words, scales):
    return unpack_weight(words.reshape(words.shape[0], 128, -1, 2), scales, "e2m1")


E, Q, J, L, K, N = 512, 4, 4, 512, 1024, 1024

T = E * Q
F = J * L


def silu(v):
    return v / (1.0 + np.exp(-v))


def setup_inputs():
    s, t = mx_kscale(K), mx_kscale(F)
    x = np.random.standard_normal((K, T)) * s[:, None]
    d = np.random.standard_normal((K, L)) / np.sqrt(K) / s[:, None]
    w = 1.5 * np.random.standard_normal((F, N)) / np.sqrt(F) / t[:, None]
    x_words, x_scales = pack4(x)
    d_words, d_scales = pack4(d)
    w_words, w_scales = pack4(w)
    return {"x_words": x_words, "x_scales": x_scales,
            "d_words": d_words, "d_scales": d_scales,
            "bias_d": bf(0.3 * np.random.standard_normal(L)),
            "rad": bf(1.0 + 0.5 * np.random.standard_normal((E, Q, L))),
            "sph": bf(np.random.standard_normal((E, Q, J)) / np.sqrt(Q)),
            "gain": bf((1.0 + 0.2 * np.random.standard_normal((J, L))) * t.reshape(J, L)),
            "w_words": w_words, "w_scales": w_scales,
            "bias_o": bf(0.3 * np.random.standard_normal(N)),
            "msg": bf(0.5 * np.random.standard_normal((E, N)))}


def reference(x_words, x_scales, d_words, d_scales, bias_d, rad, sph, gain, w_words, w_scales, bias_o, msg):
    h = unpack4(x_words, x_scales).T @ unpack4(d_words, d_scales)
    u = silu(h + f64(bias_d)).reshape(E, Q, L) * f64(rad)
    v = (f64(sph)[:, :, :, None] * u[:, :, None, :]).sum(axis=1)
    z = (v * f64(gain)).reshape(E, F)
    y = mxq(z, 1, "e4m3") @ unpack4(w_words, w_scales)
    return (f64(msg) + silu(y + f64(bias_o))) * np.sqrt(0.5)

@@ -1,0 +1,326 @@
+import math
+from contextlib import ExitStack
+
+import concourse.mybir as mybir
+from concourse.masks import make_identity
+
+E, Q, J, L, K, N = 512, 4, 4, 512, 1024, 1024
+T = E * Q
+P = 128
+F32 = mybir.dt.float32
+BF16 = mybir.dt.bfloat16
+U32 = mybir.dt.uint32
+I32 = mybir.dt.int32
+U8 = mybir.dt.uint8
+FP8X4 = mybir.dt.float8_e4m3fn_x4
+FP4X4 = mybir.dt.float4_e2m1fn_x4
+ACT = mybir.ActivationFunctionType
+ALU = mybir.AluOpType
+AX = mybir.AxisListType
+
+FLOPS = 2 * T * K * L + 2 * E * (J * L) * N
+
+G1 = K // 512
+N_TT = T // P
+N_ET = E // P
+TPE = N_TT // N_ET
+EPT = P // Q
+XC = 2 * P * TPE
+HALF = math.sqrt(0.5)
+
+
+def tile_triplet_bilinear_messages_f2_kernel(
+    tc, x_words, x_scales, d_words, d_scales, bias_d, rad, sph, gain, w_words, w_scales, bias_o, msg, out
+):
+    nc = tc.nc
+    with ExitStack() as ctx:
+        keep = ctx.enter_context(tc.tile_pool(name="keep", bufs=1))
+        work = ctx.enter_context(tc.tile_pool(name="work", bufs=3))
+        h_pool = ctx.enter_context(tc.psum_pool(name="h_pool", bufs=3))
+        v_pool = ctx.enter_context(tc.psum_pool(name="v_pool", bufs=3))
+        y_pool = ctx.enter_context(tc.psum_pool(name="y_pool", bufs=2))
+        ctx.enter_context(tc.manual_schedule())
+
+        x_w = [keep.tile([P, G1, XC], U8, align_bytes=64, name="x_w%d" % k) for k in range(N_ET)]
+        x_s = keep.tile([P, G1, T], U8, align_bytes=64, name="x_s")
+        d_w = keep.tile([P, G1, 2 * L], U8, align_bytes=64, name="d_w")
+        d_s = keep.tile([P, G1, L], U8, align_bytes=64, name="d_s")
+        w_w = keep.tile([P, J, 2 * N], U8, align_bytes=64, name="w_w")
+        w_s = keep.tile([P, J, N], U8, align_bytes=64, name="w_s")
+        rad_sb = keep.tile([P, N_TT, L], BF16, align_bytes=64, name="rad_sb")
+        sph_sb = keep.tile([P, N_TT, J], BF16, align_bytes=64, name="sph_sb")
+        gain_sb = keep.tile([P, J, 4], BF16, align_bytes=64, name="gain_sb")
+        msg_sb = keep.tile([P, N_ET, N], BF16, align_bytes=64, name="msg_sb")
+        rows = keep.tile([P, L + N], BF16, align_bytes=64, name="rows")
+        ones = keep.tile([P, P], BF16, align_bytes=64, name="ones")
+        ident = keep.tile([P, P], F32, align_bytes=64, name="ident")
+        mask = keep.tile([P, EPT], F32, align_bytes=64, name="mask")
+        mix = keep.tile([P, N_TT, P], F32, align_bytes=64, name="mix")
+        bd = keep.tile([P, L], F32, align_bytes=64, name="bd")
+        bo = keep.tile([P, N], F32, align_bytes=64, name="bo")
+        warm = keep.tile([P, 1], F32, align_bytes=64, name="warm")
+
+        nc.vector.memset(warm[:], 0.0)
+        nc.vector.memset(d_s[:].rearrange("p g n -> p (g n)").bitcast(I32), 0)
+        nc.vector.memset(rows[:].bitcast(I32), 0)
+        nc.vector.memset(x_s[:].rearrange("p g n -> p (g n)").bitcast(I32), 0)
+        nc.vector.memset(ones[:], 1.0)
+        nc.scalar.activation(out=warm[:], in_=warm[:], func=ACT.Silu)
+        make_identity(nc, ident[:])
+        nc.gpsimd.memset(w_s[:].rearrange("p g n -> p (g n)").bitcast(I32), 0)
+        nc.vector.tensor_reduce(
+            out=mask[:], in_=ident[:].rearrange("p (e q) -> p e q", q=Q), axis=AX.X, op=ALU.add
+        )
+
+        def load_scales(dst, scales):
+            for quad in range(4):
+                nc.sync.dma_start(
+                    out=dst[32 * quad : 32 * quad + 4, :, :].bitcast(I32),
+                    in_=scales[:, 4 * quad : 4 * quad + 4, :].rearrange("g r n -> r g n").bitcast(I32),
+                )
+
+        x_hbm = x_words.rearrange("g p n -> p g n")
+        rad_hbm = rad.rearrange("e q l -> (e q) l").rearrange("(t p) l -> p t l", p=P)
+        msg_hbm = msg.rearrange("(k p) n -> p k n", p=P)
+
+        def load_x(k):
+            nc.sync.dma_start(
+                out=x_w[k][:].bitcast(I32), in_=x_hbm[:, :, XC * k : XC * (k + 1)].bitcast(I32)
+            )
+
+        def load_rad(k):
+            nc.sync.dma_start(
+                out=rad_sb[:, TPE * k : TPE * (k + 1), :], in_=rad_hbm[:, TPE * k : TPE * (k + 1), :]
+            )
+
+        def load_msg(k):
+            nc.sync.dma_start(out=msg_sb[:, k, :], in_=msg_hbm[:, k, :])
+
+        nc.sync.dma_start(out=d_w[:].bitcast(I32), in_=d_words.rearrange("g p n -> p g n").bitcast(I32))
+        load_x(0)
+        load_scales(d_s, d_scales)
+        load_scales(x_s, x_scales)
+        nc.scalar.dma_start(out=rows[0:1, 0:L], in_=bias_d.rearrange("(o n) -> o n", o=1))
+        nc.scalar.dma_start(out=rows[0:1, L : L + N], in_=bias_o.rearrange("(o n) -> o n", o=1))
+        load_rad(0)
+        with nc.allow_non_contiguous_dma(reason="small constants"):
+            nc.scalar.dma_start(
+                out=sph_sb[:], in_=sph.rearrange("e q j -> (e q) j").rearrange("(t p) j -> p t j", p=P)
+            )
+            nc.scalar.dma_start(out=gain_sb[:], in_=gain.rearrange("j (m t) -> m j t", t=4))
+        load_x(1)
+        load_rad(1)
+        load_scales(w_s, w_scales)
+        nc.sync.dma_start(out=w_w[:].bitcast(I32), in_=w_words.rearrange("g p n -> p g n").bitcast(I32))
+        load_x(2)
+        load_rad(2)
+        load_msg(0)
+        load_x(3)
+        load_rad(3)
+        load_msg(1)
+        load_msg(2)
+        load_msg(3)
+
+        def spread_bias_d():
+            ps = y_pool.tile([P, L], F32, name="y")
+            nc.tensor.matmul(ps[:], ones[:], rows[:, 0:L], start=True, stop=True)
+            nc.scalar.copy(
+                out=bd[:].rearrange("p (t m) -> p t m", t=4), in_=ps[:].rearrange("p (m t) -> p t m", t=4)
+            )
+
+        def spread_bias_o():
+            for n in range(2):
+                ps = y_pool.tile([P, L], F32, name="y")
+                nc.tensor.matmul(ps[:], ones[:], rows[:, L + 512 * n : L + 512 * (n + 1)], start=True, stop=True)
+                nc.scalar.copy(out=bo[:, 512 * n : 512 * (n + 1)], in_=ps[:])
+
+        def build_mix(k):
+            nc.vector.tensor_tensor(
+                out=mix[:, TPE * k : TPE * (k + 1), :].rearrange("p t (j e) -> p (t j) e", j=J),
+                in0=mask[:].unsqueeze(1).to_broadcast([P, TPE * J, EPT]),
+                in1=sph_sb[:, TPE * k : TPE * (k + 1), :]
+                .rearrange("p t j -> p (t j)")
+                .unsqueeze(2)
+                .to_broadcast([P, TPE * J, EPT]),
+                op=ALU.mult,
+            )
+
+        h_of, hb_of, a_of, u_of, v_of = {}, {}, {}, {}, {}
+        z_of, zc_of, zs_of, y_of, ob_of, os_of = {}, {}, {}, {}, {}, {}
+
+        def stage1(t):
+            h = h_pool.tile([P, L], F32, name="h")
+            h_of[t] = h
+            for g in range(G1):
+                nc.tensor.matmul_mx(
+                    out=h[:],
+                    lhsT=x_w[t // TPE][:, g, 2 * P * (t % TPE) : 2 * P * (t % TPE + 1)].bitcast(FP4X4),
+                    lhsT_scale=x_s[:, g, P * t : P * (t + 1)],
+                    rhs=d_w[:, g, :].bitcast(FP4X4),
+                    rhs_scale=d_s[:, g, :],
+                    start=(g == 0),
+                    stop=(g == G1 - 1),
+                )
+
+        def add_bias_d(t):
+            hb = work.tile([P, L], F32, align_bytes=64, name="hb")
+            hb_of[t] = hb
+            nc.vector.tensor_tensor(
+                out=hb[:].rearrange("p (t m) -> p t m", t=4),
+                in0=h_of[t][:].rearrange("p (m t) -> p t m", t=4),
+                in1=bd[:].rearrange("p (t m) -> p t m", t=4),
+                op=ALU.add,
+            )
+
+        def silu_h(t):
+            a = work.tile([P, L], F32, align_bytes=64, name="a")
+            a_of[t] = a
+            nc.scalar.activation(out=a[:], in_=hb_of[t][:], func=ACT.Silu)
+
+        def times_rad(t):
+            u = work.tile([P, L], F32, align_bytes=64, name="u")
+            u_of[t] = u
+            engine = nc.vector if t < 2 else nc.gpsimd
+            engine.tensor_tensor(
+                out=u[:].rearrange("p (t m) -> p t m", t=4),
+                in0=a_of[t][:].rearrange("p (t m) -> p t m", t=4),
+                in1=rad_sb[:, t, :].rearrange("p (m t) -> p t m", t=4),
+                op=ALU.mult,
+            )
+
+        def fold(t):
+            v = v_pool.tile([P, 4, P], F32, name="v")
+            v_of[t] = v
+            for i in range(4):
+                nc.tensor.matmul(v[:, i, :], u_of[t][:, P * i : P * (i + 1)], mix[:, t, :], start=True, stop=True)
+
+        def times_gain(t):
+            k, q = divmod(t, TPE)
+            if q == 0:
+                z_of[k] = work.tile([P, J * P * 4], BF16, align_bytes=64, name="z", bufs=2)
+            z4 = z_of[k][:].rearrange("p (j e i) -> p j e i", j=J, i=4)
+            nc.vector.tensor_tensor(
+                out=z4[:, :, EPT * q : EPT * (q + 1), :],
+                in0=v_of[t][:].rearrange("p i (j e) -> p j e i", j=J),
+                in1=gain_sb[:].unsqueeze(2).to_broadcast([P, J, EPT, 4]),
+                op=ALU.mult,
+            )
+
+        def quantize(k, parts):
+            zc = work.tile([P, J * P], U32, align_bytes=64, name="zc", bufs=2)
+            zs = work.tile([P, J * P], U8, align_bytes=64, name="zs", bufs=2)
+            zc_of[k], zs_of[k] = zc, zs
+            w = J * P // parts
+            for i in range(parts):
+                nc.vector.quantize_mx(
+                    out=zc[:, w * i : w * (i + 1)].bitcast(FP8X4),
+                    scales=zs[:, w * i : w * (i + 1)],
+                    in_=z_of[k][:, 4 * w * i : 4 * w * (i + 1)],
+                )
+
+        def stage2(k, n, j):
+            if j == 0:
+                y_of[k, n] = y_pool.tile([P, 512], F32, name="y")
+            nc.tensor.matmul_mx(
+                out=y_of[k, n][:],
+                lhsT=zc_of[k][:, P * j : P * (j + 1)].bitcast(FP8X4),
+                lhsT_scale=zs_of[k][:, P * j : P * (j + 1)],
+                rhs=w_w[:, j, 1024 * n : 1024 * (n + 1)].bitcast(FP4X4),
+                rhs_scale=w_s[:, j, 512 * n : 512 * (n + 1)],
+                start=(j == 0),
+                stop=(j == J - 1),
+            )
+
+        def add_bias_o(k, n):
+            ob = work.tile([P, 512], F32, align_bytes=64, name="ob")
+            ob_of[k, n] = ob
+            nc.vector.tensor_tensor(out=ob[:], in0=y_of[k, n][:], in1=bo[:, 512 * n : 512 * (n + 1)], op=ALU.add)
+
+        def silu_y(k, n):
+            so = work.tile([P, 512], F32, align_bytes=64, name="so")
+            os_of[k, n] = so
+            nc.scalar.activation(out=so[:], in_=ob_of[k, n][:], func=ACT.Silu)
+
+        def add_msg(k, n):
+            r = work.tile([P, 512], F32, align_bytes=64, name="r")
+            os_of[k, n, "r"] = r
+            nc.gpsimd.tensor_tensor(
+                out=r[:], in0=os_of[k, n][:], in1=msg_sb[:, k, 512 * n : 512 * (n + 1)], op=ALU.add
+            )
+
+        def finish(k, n):
+            o = work.tile([P, 512], F32, align_bytes=64, name="o")
+            nc.scalar.activation(out=o[:], in_=os_of[k, n, "r"][:], func=ACT.Copy, scale=HALF)
+            nc.sync.dma_start(out=out[P * k : P * (k + 1), 512 * n : 512 * (n + 1)], in_=o[:])
+
+        mc = keep.tile([P, N], F32, align_bytes=64, name="mc")
+
+        def last_output(n, lo, hi):
+            k = N_ET - 1
+            cols = slice(512 * n + lo, 512 * n + hi)
+            ob = work.tile([P, hi - lo], F32, align_bytes=64, name="ob")
+            so = work.tile([P, hi - lo], F32, align_bytes=64, name="so")
+            o = work.tile([P, hi - lo], F32, align_bytes=64, name="o")
+            nc.vector.tensor_tensor(out=ob[:], in0=y_of[k, n][:, lo:hi], in1=bo[:, cols], op=ALU.add)
+            nc.scalar.activation(out=so[:], in_=ob[:], func=ACT.Silu)
+            return lambda: (
+                nc.vector.scalar_tensor_tensor(
+                    out=o[:], in0=so[:], scalar=HALF, in1=mc[:, cols], op0=ALU.mult, op1=ALU.add
+                ),
+                nc.sync.dma_start(out=out[P * k : P * (k + 1), cols], in_=o[:]),
+            )
+
+        todo = []
+        done1, done2 = [], []
+        for step in range(N_TT + 3):
+            t1, t2 = step, step - 2
+            if t1 < N_TT:
+                stage1(t1)
+            if step == 0:
+                spread_bias_d()
+            if step == 2:
+                spread_bias_o()
+            if 0 <= t2 < N_TT:
+                fold(t2)
+            take = 2 if t1 < N_TT else 4
+            finished = []
+            for k, n, j in todo[:take]:
+                stage2(k, n, j)
+                if j == J - 1:
+                    finished.append((k, n))
+            todo = todo[take:]
+
+            if t1 < N_TT:
+                add_bias_d(t1)
+                silu_h(t1)
+                if step == 0:
+                    build_mix(0)
+                times_rad(t1)
+            for k, n in done1:
+                add_bias_o(k, n)
+                silu_y(k, n)
+                add_msg(k, n)
+            for k, n in done2:
+                finish(k, n)
+            done2 = done1
+            done1 = finished
+            if 0 <= t2 < N_TT:
+                times_gain(t2)
+                if t2 % TPE == TPE - 1:
+                    k = t2 // TPE
+                    quantize(k, 1 if k < N_ET - 1 else 2)
+                    if k < N_ET - 1:
+                        todo.extend((k, n, j) for n in range(2) for j in range(J))
+            if step in (2, 4, 6):
+                build_mix(step // 2)
+            if step == 12:
+                nc.scalar.activation(out=mc[:], in_=msg_sb[:, N_ET - 1, :], func=ACT.Copy, scale=HALF)
+        late = []
+        for n in range(2):
+            for j in range(J):
+                stage2(N_ET - 1, n, j)
+            for lo in (0, 256):
+                late.append(last_output(n, lo, lo + 256))
+                if len(late) > 1:
+                    late[-2]()
+        late[-1]()

@@ -27,6 +27,7 @@ TPE = N_TT // N_ET
 EPT = P // Q
 XC = 2 * P * TPE
 HALF = math.sqrt(0.5)
+LAG = 4
 
 
 def tile_triplet_bilinear_messages_f2_kernel(
@@ -42,16 +43,18 @@ def tile_triplet_bilinear_messages_f2_kernel(
         ctx.enter_context(tc.manual_schedule())
 
         x_w = [keep.tile([P, G1, XC], U8, align_bytes=64, name="x_w%d" % k) for k in range(N_ET)]
-        x_s = keep.tile([P, G1, T], U8, align_bytes=64, name="x_s")
+        x_s0 = keep.tile([P, G1, P * TPE], U8, align_bytes=64, name="x_s0")
+        x_s1 = keep.tile([P, G1, T - P * TPE], U8, align_bytes=64, name="x_s1")
         d_w = keep.tile([P, G1, 2 * L], U8, align_bytes=64, name="d_w")
         d_s = keep.tile([P, G1, L], U8, align_bytes=64, name="d_s")
         w_w = keep.tile([P, J, 2 * N], U8, align_bytes=64, name="w_w")
         w_s = keep.tile([P, J, N], U8, align_bytes=64, name="w_s")
         rad_sb = keep.tile([P, N_TT, L], BF16, align_bytes=64, name="rad_sb")
-        sph_sb = keep.tile([P, N_TT, J], BF16, align_bytes=64, name="sph_sb")
+        sph_sb = [keep.tile([P, TPE, J], BF16, align_bytes=64, name="sph_sb%d" % k) for k in range(N_ET)]
         gain_sb = keep.tile([P, J, 4], BF16, align_bytes=64, name="gain_sb")
         msg_sb = keep.tile([P, N_ET, N], BF16, align_bytes=64, name="msg_sb")
-        rows = keep.tile([P, L + N], BF16, align_bytes=64, name="rows")
+        row_d = keep.tile([P, L], BF16, align_bytes=64, name="row_d")
+        row_o = keep.tile([P, N], BF16, align_bytes=64, name="row_o")
         ones = keep.tile([P, P], BF16, align_bytes=64, name="ones")
         ident = keep.tile([P, P], F32, align_bytes=64, name="ident")
         mask = keep.tile([P, EPT], F32, align_bytes=64, name="mask")
@@ -60,17 +63,33 @@ def tile_triplet_bilinear_messages_f2_kernel(
         bo = keep.tile([P, N], F32, align_bytes=64, name="bo")
         warm = keep.tile([P, 1], F32, align_bytes=64, name="warm")
 
-        nc.vector.memset(warm[:], 0.0)
-        nc.vector.memset(d_s[:].rearrange("p g n -> p (g n)").bitcast(I32), 0)
-        nc.vector.memset(rows[:].bitcast(I32), 0)
-        nc.vector.memset(x_s[:].rearrange("p g n -> p (g n)").bitcast(I32), 0)
-        nc.vector.memset(ones[:], 1.0)
-        nc.scalar.activation(out=warm[:], in_=warm[:], func=ACT.Silu)
+        def zero(tile_words):
+            nc.vector.memset(tile_words.bitcast(I32), 0)
+
+        x_hbm = x_words.rearrange("g p n -> p g n")
+        sph_hbm = sph.rearrange("e q j -> (e q) j").rearrange("(t p) j -> p t j", p=P)
+
+        def load_sph(engine, k):
+            with nc.allow_non_contiguous_dma(reason="8-byte rows"):
+                engine.dma_start(out=sph_sb[k][:], in_=sph_hbm[:, TPE * k : TPE * (k + 1), :])
+
+        nc.gpsimd.dma_start(out=x_w[0][:].bitcast(I32), in_=x_hbm[:, :, 0:XC].bitcast(I32))
+        load_sph(nc.gpsimd, 0)
         make_identity(nc, ident[:])
-        nc.gpsimd.memset(w_s[:].rearrange("p g n -> p (g n)").bitcast(I32), 0)
+        nc.scalar.dma_start(out=d_w[:].bitcast(I32), in_=d_words.rearrange("g p n -> p g n").bitcast(I32))
+        zero(row_d[:])
+        zero(d_s[:].rearrange("p g n -> p (g n)"))
+        zero(x_s0[:].rearrange("p g n -> p (g n)"))
+        nc.vector.memset(ones[:], 1.0)
+        nc.vector.memset(warm[:], 0.0)
+        zero(x_s1[:].rearrange("p g n -> p (g n)"))
         nc.vector.tensor_reduce(
             out=mask[:], in_=ident[:].rearrange("p (e q) -> p e q", q=Q), axis=AX.X, op=ALU.add
         )
+        zero(w_s[:].rearrange("p g n -> p (g n)"))
+        zero(row_o[:])
+        nc.scalar.dma_start(out=row_d[0:1, :], in_=bias_d.rearrange("(o n) -> o n", o=1))
+        nc.scalar.activation(out=warm[:], in_=warm[:], func=ACT.Silu)
 
         def load_scales(dst, scales):
             for quad in range(4):
@@ -79,14 +98,11 @@ def tile_triplet_bilinear_messages_f2_kernel(
                     in_=scales[:, 4 * quad : 4 * quad + 4, :].rearrange("g r n -> r g n").bitcast(I32),
                 )
 
-        x_hbm = x_words.rearrange("g p n -> p g n")
         rad_hbm = rad.rearrange("e q l -> (e q) l").rearrange("(t p) l -> p t l", p=P)
         msg_hbm = msg.rearrange("(k p) n -> p k n", p=P)
 
         def load_x(k):
-            nc.sync.dma_start(
-                out=x_w[k][:].bitcast(I32), in_=x_hbm[:, :, XC * k : XC * (k + 1)].bitcast(I32)
-            )
+            nc.sync.dma_start(out=x_w[k][:].bitcast(I32), in_=x_hbm[:, :, XC * k : XC * (k + 1)].bitcast(I32))
 
         def load_rad(k):
             nc.sync.dma_start(
@@ -96,26 +112,24 @@ def tile_triplet_bilinear_messages_f2_kernel(
         def load_msg(k):
             nc.sync.dma_start(out=msg_sb[:, k, :], in_=msg_hbm[:, k, :])
 
-        nc.sync.dma_start(out=d_w[:].bitcast(I32), in_=d_words.rearrange("g p n -> p g n").bitcast(I32))
-        load_x(0)
         load_scales(d_s, d_scales)
-        load_scales(x_s, x_scales)
-        nc.scalar.dma_start(out=rows[0:1, 0:L], in_=bias_d.rearrange("(o n) -> o n", o=1))
-        nc.scalar.dma_start(out=rows[0:1, L : L + N], in_=bias_o.rearrange("(o n) -> o n", o=1))
+        load_scales(x_s0, x_scales[:, :, 0 : P * TPE])
         load_rad(0)
-        with nc.allow_non_contiguous_dma(reason="small constants"):
-            nc.scalar.dma_start(
-                out=sph_sb[:], in_=sph.rearrange("e q j -> (e q) j").rearrange("(t p) j -> p t j", p=P)
-            )
-            nc.scalar.dma_start(out=gain_sb[:], in_=gain.rearrange("j (m t) -> m j t", t=4))
         load_x(1)
+        load_sph(nc.sync, 1)
+        load_scales(x_s1, x_scales[:, :, P * TPE : T])
+        with nc.allow_non_contiguous_dma(reason="small constants"):
+            nc.sync.dma_start(out=gain_sb[:], in_=gain.rearrange("j (m t) -> m j t", t=4))
         load_rad(1)
+        nc.sync.dma_start(out=row_o[0:1, :], in_=bias_o.rearrange("(o n) -> o n", o=1))
+        load_x(2)
+        load_sph(nc.sync, 2)
+        load_sph(nc.sync, 3)
         load_scales(w_s, w_scales)
         nc.sync.dma_start(out=w_w[:].bitcast(I32), in_=w_words.rearrange("g p n -> p g n").bitcast(I32))
-        load_x(2)
         load_rad(2)
-        load_msg(0)
         load_x(3)
+        load_msg(0)
         load_rad(3)
         load_msg(1)
         load_msg(2)
@@ -123,7 +137,7 @@ def tile_triplet_bilinear_messages_f2_kernel(
 
         def spread_bias_d():
             ps = y_pool.tile([P, L], F32, name="y")
-            nc.tensor.matmul(ps[:], ones[:], rows[:, 0:L], start=True, stop=True)
+            nc.tensor.matmul(ps[:], ones[:], row_d[:], start=True, stop=True)
             nc.scalar.copy(
                 out=bd[:].rearrange("p (t m) -> p t m", t=4), in_=ps[:].rearrange("p (m t) -> p t m", t=4)
             )
@@ -131,14 +145,14 @@ def tile_triplet_bilinear_messages_f2_kernel(
         def spread_bias_o():
             for n in range(2):
                 ps = y_pool.tile([P, L], F32, name="y")
-                nc.tensor.matmul(ps[:], ones[:], rows[:, L + 512 * n : L + 512 * (n + 1)], start=True, stop=True)
+                nc.tensor.matmul(ps[:], ones[:], row_o[:, 512 * n : 512 * (n + 1)], start=True, stop=True)
                 nc.scalar.copy(out=bo[:, 512 * n : 512 * (n + 1)], in_=ps[:])
 
         def build_mix(k):
             nc.vector.tensor_tensor(
                 out=mix[:, TPE * k : TPE * (k + 1), :].rearrange("p t (j e) -> p (t j) e", j=J),
                 in0=mask[:].unsqueeze(1).to_broadcast([P, TPE * J, EPT]),
-                in1=sph_sb[:, TPE * k : TPE * (k + 1), :]
+                in1=sph_sb[k][:]
                 .rearrange("p t j -> p (t j)")
                 .unsqueeze(2)
                 .to_broadcast([P, TPE * J, EPT]),
@@ -151,11 +165,12 @@ def tile_triplet_bilinear_messages_f2_kernel(
         def stage1(t):
             h = h_pool.tile([P, L], F32, name="h")
             h_of[t] = h
+            scale_plane, col = (x_s0, P * t) if t < TPE else (x_s1, P * (t - TPE))
             for g in range(G1):
                 nc.tensor.matmul_mx(
                     out=h[:],
                     lhsT=x_w[t // TPE][:, g, 2 * P * (t % TPE) : 2 * P * (t % TPE + 1)].bitcast(FP4X4),
-                    lhsT_scale=x_s[:, g, P * t : P * (t + 1)],
+                    lhsT_scale=scale_plane[:, g, col : col + P],
                     rhs=d_w[:, g, :].bitcast(FP4X4),
                     rhs_scale=d_s[:, g, :],
                     start=(g == 0),
@@ -178,9 +193,9 @@ def tile_triplet_bilinear_messages_f2_kernel(
             nc.scalar.activation(out=a[:], in_=hb_of[t][:], func=ACT.Silu)
 
         def times_rad(t):
-            u = work.tile([P, L], F32, align_bytes=64, name="u")
+            u = work.tile([P, L], F32, align_bytes=64, name="u", bufs=LAG + 3)
             u_of[t] = u
-            engine = nc.vector if t < 2 else nc.gpsimd
+            engine = nc.vector if t < 1 else nc.gpsimd
             engine.tensor_tensor(
                 out=u[:].rearrange("p (t m) -> p t m", t=4),
                 in0=a_of[t][:].rearrange("p (t m) -> p t m", t=4),
@@ -194,17 +209,20 @@ def tile_triplet_bilinear_messages_f2_kernel(
             for i in range(4):
                 nc.tensor.matmul(v[:, i, :], u_of[t][:, P * i : P * (i + 1)], mix[:, t, :], start=True, stop=True)
 
-        def times_gain(t):
+        def times_gain(t, parts):
             k, q = divmod(t, TPE)
             if q == 0:
                 z_of[k] = work.tile([P, J * P * 4], BF16, align_bytes=64, name="z", bufs=2)
             z4 = z_of[k][:].rearrange("p (j e i) -> p j e i", j=J, i=4)
-            nc.vector.tensor_tensor(
-                out=z4[:, :, EPT * q : EPT * (q + 1), :],
-                in0=v_of[t][:].rearrange("p i (j e) -> p j e i", j=J),
-                in1=gain_sb[:].unsqueeze(2).to_broadcast([P, J, EPT, 4]),
-                op=ALU.mult,
-            )
+            jp = J // parts
+            for i in range(parts):
+                js = slice(jp * i, jp * (i + 1))
+                nc.vector.tensor_tensor(
+                    out=z4[:, js, EPT * q : EPT * (q + 1), :],
+                    in0=v_of[t][:].rearrange("p i (j e) -> p j e i", j=J)[:, js, :, :],
+                    in1=gain_sb[:, js, :].unsqueeze(2).to_broadcast([P, jp, EPT, 4]),
+                    op=ALU.mult,
+                )
 
         def quantize(k, parts):
             zc = work.tile([P, J * P], U32, align_bytes=64, name="zc", bufs=2)
@@ -232,12 +250,12 @@ def tile_triplet_bilinear_messages_f2_kernel(
             )
 
         def add_bias_o(k, n):
-            ob = work.tile([P, 512], F32, align_bytes=64, name="ob")
+            ob = work.tile([P, 512], F32, align_bytes=64, name="ob", bufs=4)
             ob_of[k, n] = ob
             nc.vector.tensor_tensor(out=ob[:], in0=y_of[k, n][:], in1=bo[:, 512 * n : 512 * (n + 1)], op=ALU.add)
 
         def silu_y(k, n):
-            so = work.tile([P, 512], F32, align_bytes=64, name="so")
+            so = work.tile([P, 512], F32, align_bytes=64, name="so", bufs=4)
             os_of[k, n] = so
             nc.scalar.activation(out=so[:], in_=ob_of[k, n][:], func=ACT.Silu)
 
@@ -249,53 +267,55 @@ def tile_triplet_bilinear_messages_f2_kernel(
             )
 
         def finish(k, n):
-            o = work.tile([P, 512], F32, align_bytes=64, name="o")
+            o = work.tile([P, 512], F32, align_bytes=64, name="o", bufs=6)
             nc.scalar.activation(out=o[:], in_=os_of[k, n, "r"][:], func=ACT.Copy, scale=HALF)
             nc.sync.dma_start(out=out[P * k : P * (k + 1), 512 * n : 512 * (n + 1)], in_=o[:])
 
-        mc = keep.tile([P, N], F32, align_bytes=64, name="mc")
+        mc = {k: keep.tile([P, N], F32, align_bytes=64, name="mc%d" % k) for k in (N_ET - 2, N_ET - 1)}
 
-        def last_output(n, lo, hi):
-            k = N_ET - 1
+        def last_output(k, n, lo, hi):
             cols = slice(512 * n + lo, 512 * n + hi)
-            ob = work.tile([P, hi - lo], F32, align_bytes=64, name="ob")
-            so = work.tile([P, hi - lo], F32, align_bytes=64, name="so")
-            o = work.tile([P, hi - lo], F32, align_bytes=64, name="o")
+            ob = work.tile([P, hi - lo], F32, align_bytes=64, name="ob", bufs=4)
+            so = work.tile([P, hi - lo], F32, align_bytes=64, name="so", bufs=4)
+            o = work.tile([P, hi - lo], F32, align_bytes=64, name="o", bufs=6)
             nc.vector.tensor_tensor(out=ob[:], in0=y_of[k, n][:, lo:hi], in1=bo[:, cols], op=ALU.add)
             nc.scalar.activation(out=so[:], in_=ob[:], func=ACT.Silu)
             return lambda: (
                 nc.vector.scalar_tensor_tensor(
-                    out=o[:], in0=so[:], scalar=HALF, in1=mc[:, cols], op0=ALU.mult, op1=ALU.add
+                    out=o[:], in0=so[:], scalar=HALF, in1=mc[k][:, cols], op0=ALU.mult, op1=ALU.add
                 ),
                 nc.sync.dma_start(out=out[P * k : P * (k + 1), cols], in_=o[:]),
             )
 
         todo = []
         done1, done2 = [], []
-        for step in range(N_TT + 3):
-            t1, t2 = step, step - 2
-            if t1 < N_TT:
-                stage1(t1)
+        for step in range(N_TT + LAG):
+            t1, t2 = step, step - LAG
             if step == 0:
                 spread_bias_d()
-            if step == 2:
-                spread_bias_o()
+                build_mix(0)
+            if t1 < N_TT:
+                stage1(t1)
             if 0 <= t2 < N_TT:
                 fold(t2)
-            take = 2 if t1 < N_TT else 4
+            if step == LAG:
+                spread_bias_o()
             finished = []
-            for k, n, j in todo[:take]:
+            for k, n, j in todo[:2]:
+                if k == N_ET - 2 and n == 1:
+                    break
                 stage2(k, n, j)
+                todo = todo[1:]
                 if j == J - 1:
                     finished.append((k, n))
-            todo = todo[take:]
 
             if t1 < N_TT:
                 add_bias_d(t1)
                 silu_h(t1)
-                if step == 0:
-                    build_mix(0)
-                times_rad(t1)
+                if t1 >= 1:
+                    times_rad(t1)
+                if t1 == 1:
+                    times_rad(0)
             for k, n in done1:
                 add_bias_o(k, n)
                 silu_y(k, n)
@@ -305,22 +325,31 @@ def tile_triplet_bilinear_messages_f2_kernel(
             done2 = done1
             done1 = finished
             if 0 <= t2 < N_TT:
-                times_gain(t2)
+                times_gain(t2, 1 if t2 < N_TT - 1 else 2)
                 if t2 % TPE == TPE - 1:
                     k = t2 // TPE
                     quantize(k, 1 if k < N_ET - 1 else 2)
                     if k < N_ET - 1:
                         todo.extend((k, n, j) for n in range(2) for j in range(J))
-            if step in (2, 4, 6):
-                build_mix(step // 2)
-            if step == 12:
-                nc.scalar.activation(out=mc[:], in_=msg_sb[:, N_ET - 1, :], func=ACT.Copy, scale=HALF)
-        late = []
-        for n in range(2):
+            if step in (3, 5, 7):
+                build_mix((step - 1) // 2)
+            if step == 11:
+                cols = slice(512, 1024)
+                nc.scalar.activation(
+                    out=mc[N_ET - 2][:, cols], in_=msg_sb[:, N_ET - 2, cols], func=ACT.Copy, scale=HALF
+                )
+            if step in (12, 13):
+                cols = slice(512 * (step - 12), 512 * (step - 11))
+                nc.scalar.activation(
+                    out=mc[N_ET - 1][:, cols], in_=msg_sb[:, N_ET - 1, cols], func=ACT.Copy, scale=HALF
+                )
+        waiting = []
+        for k, n in ((N_ET - 2, 1), (N_ET - 1, 0), (N_ET - 1, 1)):
             for j in range(J):
-                stage2(N_ET - 1, n, j)
-            for lo in (0, 256):
-                late.append(last_output(n, lo, lo + 256))
-                if len(late) > 1:
-                    late[-2]()
-        late[-1]()
+                stage2(k, n, j)
+            halves = [last_output(k, n, lo, lo + 256) for lo in (0, 256)]
+            for last in waiting:
+                last()
+            waiting = halves
+        for last in waiting:
+            last()

@@ -28,6 +28,7 @@ EPT = P // Q
 XC = 2 * P * TPE
 HALF = math.sqrt(0.5)
 LAG = 4
+WARM = 20
 
 
 def tile_triplet_bilinear_messages_f2_kernel(
@@ -63,6 +64,13 @@ def tile_triplet_bilinear_messages_f2_kernel(
         bo = keep.tile([P, N], F32, align_bytes=64, name="bo")
         warm = keep.tile([P, 1], F32, align_bytes=64, name="warm")
 
+        def load_scales(dst, scales):
+            for quad in range(4):
+                nc.sync.dma_start(
+                    out=dst[32 * quad : 32 * quad + 4, :, :].bitcast(I32),
+                    in_=scales[:, 4 * quad : 4 * quad + 4, :].rearrange("g r n -> r g n").bitcast(I32),
+                )
+
         def zero(tile_words):
             nc.vector.memset(tile_words.bitcast(I32), 0)
 
@@ -73,30 +81,24 @@ def tile_triplet_bilinear_messages_f2_kernel(
             with nc.allow_non_contiguous_dma(reason="8-byte rows"):
                 engine.dma_start(out=sph_sb[k][:], in_=sph_hbm[:, TPE * k : TPE * (k + 1), :])
 
+        nc.gpsimd.memset(d_s[:].rearrange("p g n -> p (g n)").bitcast(I32), 0)
         nc.gpsimd.dma_start(out=x_w[0][:].bitcast(I32), in_=x_hbm[:, :, 0:XC].bitcast(I32))
         load_sph(nc.gpsimd, 0)
         make_identity(nc, ident[:])
-        nc.scalar.dma_start(out=d_w[:].bitcast(I32), in_=d_words.rearrange("g p n -> p g n").bitcast(I32))
-        zero(row_d[:])
-        zero(d_s[:].rearrange("p g n -> p (g n)"))
         zero(x_s0[:].rearrange("p g n -> p (g n)"))
+        zero(row_d[:])
         nc.vector.memset(ones[:], 1.0)
         nc.vector.memset(warm[:], 0.0)
+        load_scales(d_s, d_scales)
+        nc.scalar.dma_start(out=d_w[:].bitcast(I32), in_=d_words.rearrange("g p n -> p g n").bitcast(I32))
         zero(x_s1[:].rearrange("p g n -> p (g n)"))
         nc.vector.tensor_reduce(
             out=mask[:], in_=ident[:].rearrange("p (e q) -> p e q", q=Q), axis=AX.X, op=ALU.add
         )
-        zero(w_s[:].rearrange("p g n -> p (g n)"))
         zero(row_o[:])
+        nc.gpsimd.memset(w_s[:].rearrange("p g n -> p (g n)").bitcast(I32), 0)
         nc.scalar.dma_start(out=row_d[0:1, :], in_=bias_d.rearrange("(o n) -> o n", o=1))
         nc.scalar.activation(out=warm[:], in_=warm[:], func=ACT.Silu)
-
-        def load_scales(dst, scales):
-            for quad in range(4):
-                nc.sync.dma_start(
-                    out=dst[32 * quad : 32 * quad + 4, :, :].bitcast(I32),
-                    in_=scales[:, 4 * quad : 4 * quad + 4, :].rearrange("g r n -> r g n").bitcast(I32),
-                )
 
         rad_hbm = rad.rearrange("e q l -> (e q) l").rearrange("(t p) l -> p t l", p=P)
         msg_hbm = msg.rearrange("(k p) n -> p k n", p=P)
@@ -112,21 +114,20 @@ def tile_triplet_bilinear_messages_f2_kernel(
         def load_msg(k):
             nc.sync.dma_start(out=msg_sb[:, k, :], in_=msg_hbm[:, k, :])
 
-        load_scales(d_s, d_scales)
         load_scales(x_s0, x_scales[:, :, 0 : P * TPE])
         load_rad(0)
-        load_x(1)
-        load_sph(nc.sync, 1)
         load_scales(x_s1, x_scales[:, :, P * TPE : T])
+        load_x(1)
+        nc.sync.dma_start(out=row_o[0:1, :], in_=bias_o.rearrange("(o n) -> o n", o=1))
+        load_sph(nc.sync, 1)
         with nc.allow_non_contiguous_dma(reason="small constants"):
             nc.sync.dma_start(out=gain_sb[:], in_=gain.rearrange("j (m t) -> m j t", t=4))
         load_rad(1)
-        nc.sync.dma_start(out=row_o[0:1, :], in_=bias_o.rearrange("(o n) -> o n", o=1))
         load_x(2)
-        load_sph(nc.sync, 2)
-        load_sph(nc.sync, 3)
         load_scales(w_s, w_scales)
         nc.sync.dma_start(out=w_w[:].bitcast(I32), in_=w_words.rearrange("g p n -> p g n").bitcast(I32))
+        load_sph(nc.sync, 2)
+        load_sph(nc.sync, 3)
         load_rad(2)
         load_x(3)
         load_msg(0)
@@ -134,6 +135,11 @@ def tile_triplet_bilinear_messages_f2_kernel(
         load_msg(1)
         load_msg(2)
         load_msg(3)
+
+        def warm_up():
+            ps = y_pool.tile([P, P], F32, name="y")
+            for i in range(WARM):
+                nc.tensor.matmul(ps[:], ones[:], ones[:], start=True, stop=True)
 
         def spread_bias_d():
             ps = y_pool.tile([P, L], F32, name="y")
@@ -159,6 +165,19 @@ def tile_triplet_bilinear_messages_f2_kernel(
                 op=ALU.mult,
             )
 
+        def build_mix_piece(k, i):
+            if i == 0:
+                sph_f[k] = keep.tile([P, TPE * J], F32, align_bytes=64, name="sph_f%d" % k)
+                nc.scalar.copy(out=sph_f[k][:], in_=sph_sb[k][:].rearrange("p t j -> p (t j)"))
+            for j in range(J):
+                nc.scalar.activation(
+                    out=mix[:, TPE * k + i, EPT * j : EPT * (j + 1)],
+                    in_=mask[:],
+                    func=ACT.Copy,
+                    scale=sph_f[k][:, J * i + j : J * i + j + 1],
+                )
+
+        sph_f = {}
         h_of, hb_of, a_of, u_of, v_of = {}, {}, {}, {}, {}
         z_of, zc_of, zs_of, y_of, ob_of, os_of = {}, {}, {}, {}, {}, {}
 
@@ -288,18 +307,18 @@ def tile_triplet_bilinear_messages_f2_kernel(
             )
 
         todo = []
-        done1, done2 = [], []
+        done1, done2, done3 = [], [], []
         for step in range(N_TT + LAG):
             t1, t2 = step, step - LAG
             if step == 0:
+                warm_up()
                 spread_bias_d()
-                build_mix(0)
             if t1 < N_TT:
                 stage1(t1)
+            if t2 == 0:
+                spread_bias_o()
             if 0 <= t2 < N_TT:
                 fold(t2)
-            if step == LAG:
-                spread_bias_o()
             finished = []
             for k, n, j in todo[:2]:
                 if k == N_ET - 2 and n == 1:
@@ -315,13 +334,15 @@ def tile_triplet_bilinear_messages_f2_kernel(
                 if t1 >= 1:
                     times_rad(t1)
                 if t1 == 1:
+                    build_mix(0)
                     times_rad(0)
             for k, n in done1:
                 add_bias_o(k, n)
                 silu_y(k, n)
                 add_msg(k, n)
-            for k, n in done2:
+            for k, n in done3:
                 finish(k, n)
+            done3 = done2
             done2 = done1
             done1 = finished
             if 0 <= t2 < N_TT:
@@ -331,8 +352,8 @@ def tile_triplet_bilinear_messages_f2_kernel(
                     quantize(k, 1 if k < N_ET - 1 else 2)
                     if k < N_ET - 1:
                         todo.extend((k, n, j) for n in range(2) for j in range(J))
-            if step in (3, 5, 7):
-                build_mix((step - 1) // 2)
+            if 3 <= step < 3 + N_TT - TPE:
+                build_mix_piece(*divmod(step - 3 + TPE, TPE))
             if step == 11:
                 cols = slice(512, 1024)
                 nc.scalar.activation(
@@ -343,6 +364,8 @@ def tile_triplet_bilinear_messages_f2_kernel(
                 nc.scalar.activation(
                     out=mc[N_ET - 1][:, cols], in_=msg_sb[:, N_ET - 1, cols], func=ACT.Copy, scale=HALF
                 )
+        for k, n in done3:
+            finish(k, n)
         waiting = []
         for k, n in ((N_ET - 2, 1), (N_ET - 1, 0), (N_ET - 1, 1)):
             for j in range(J):

@@ -6,7 +6,7 @@ from concourse.masks import make_identity
 
 E, Q, J, L, K, N = 512, 4, 4, 512, 1024, 1024
 T = E * Q
-P = 128
+
 F32 = mybir.dt.float32
 BF16 = mybir.dt.bfloat16
 U32 = mybir.dt.uint32
@@ -16,19 +16,26 @@ FP8X4 = mybir.dt.float8_e4m3fn_x4
 FP4X4 = mybir.dt.float4_e2m1fn_x4
 ACT = mybir.ActivationFunctionType
 ALU = mybir.AluOpType
-AX = mybir.AxisListType
 
 FLOPS = 2 * T * K * L + 2 * E * (J * L) * N
 
-G1 = K // 512
-N_TT = T // P
-N_ET = E // P
-TPE = N_TT // N_ET
-EPT = P // Q
-XC = 2 * P * TPE
-HALF = math.sqrt(0.5)
+P = 128
+PACK = 4
+GROUPS = K // (P * PACK)
+BANK = 512
+TILES = T // P
+EDGE_TILES = E // P
+PER_EDGE_TILE = TILES // EDGE_TILES
+EDGES = P // Q
+HALVES = N // BANK
+CODE_BYTES = 2
+X_BYTES = CODE_BYTES * P * PER_EDGE_TILE
+X_COLS = P * PER_EDGE_TILE
+HALF_ROOT = math.sqrt(0.5)
+
 LAG = 4
-WARM = 20
+STEPS = TILES + LAG
+WARM_UP = 10
 
 
 def tile_triplet_bilinear_messages_f2_kernel(
@@ -43,93 +50,115 @@ def tile_triplet_bilinear_messages_f2_kernel(
         y_pool = ctx.enter_context(tc.psum_pool(name="y_pool", bufs=2))
         ctx.enter_context(tc.manual_schedule())
 
-        x_w = [keep.tile([P, G1, XC], U8, align_bytes=64, name="x_w%d" % k) for k in range(N_ET)]
-        x_s0 = keep.tile([P, G1, P * TPE], U8, align_bytes=64, name="x_s0")
-        x_s1 = keep.tile([P, G1, T - P * TPE], U8, align_bytes=64, name="x_s1")
-        d_w = keep.tile([P, G1, 2 * L], U8, align_bytes=64, name="d_w")
-        d_s = keep.tile([P, G1, L], U8, align_bytes=64, name="d_s")
-        w_w = keep.tile([P, J, 2 * N], U8, align_bytes=64, name="w_w")
+        x_w = [keep.tile([P, GROUPS, X_BYTES], U8, align_bytes=64, name="x_w%d" % k) for k in range(EDGE_TILES)]
+        x_s_first = keep.tile([P, GROUPS, X_COLS], U8, align_bytes=64, name="x_s_first")
+        x_s_rest = keep.tile([P, GROUPS, T - X_COLS], U8, align_bytes=64, name="x_s_rest")
+        d_w = keep.tile([P, GROUPS, CODE_BYTES * L], U8, align_bytes=64, name="d_w")
+        d_s = keep.tile([P, GROUPS, L], U8, align_bytes=64, name="d_s")
+        w_w = keep.tile([P, J, CODE_BYTES * N], U8, align_bytes=64, name="w_w")
         w_s = keep.tile([P, J, N], U8, align_bytes=64, name="w_s")
-        rad_sb = keep.tile([P, N_TT, L], BF16, align_bytes=64, name="rad_sb")
-        sph_sb = [keep.tile([P, TPE, J], BF16, align_bytes=64, name="sph_sb%d" % k) for k in range(N_ET)]
-        gain_sb = keep.tile([P, J, 4], BF16, align_bytes=64, name="gain_sb")
-        msg_sb = keep.tile([P, N_ET, N], BF16, align_bytes=64, name="msg_sb")
+
+        rad_sb = keep.tile([P, TILES, L], BF16, align_bytes=64, name="rad_sb")
+        sph_sb = [keep.tile([P, PER_EDGE_TILE, J], BF16, align_bytes=64, name="sph_sb%d" % k) for k in range(EDGE_TILES)]
+        sph_f32 = {}
+        gain_sb = keep.tile([P, J, PACK], BF16, align_bytes=64, name="gain_sb")
+        msg_sb = keep.tile([P, EDGE_TILES, N], BF16, align_bytes=64, name="msg_sb")
+        msg_half = {
+            k: keep.tile([P, N], F32, align_bytes=64, name="msg_half%d" % k) for k in (EDGE_TILES - 2, EDGE_TILES - 1)
+        }
         row_d = keep.tile([P, L], BF16, align_bytes=64, name="row_d")
         row_o = keep.tile([P, N], BF16, align_bytes=64, name="row_o")
         ones = keep.tile([P, P], BF16, align_bytes=64, name="ones")
-        ident = keep.tile([P, P], F32, align_bytes=64, name="ident")
-        mask = keep.tile([P, EPT], F32, align_bytes=64, name="mask")
-        mix = keep.tile([P, N_TT, P], F32, align_bytes=64, name="mix")
-        bd = keep.tile([P, L], F32, align_bytes=64, name="bd")
-        bo = keep.tile([P, N], F32, align_bytes=64, name="bo")
-        warm = keep.tile([P, 1], F32, align_bytes=64, name="warm")
+        bias_d_all = keep.tile([P, L], F32, align_bytes=64, name="bias_d_all")
+        bias_o_all = keep.tile([P, N], F32, align_bytes=64, name="bias_o_all")
+        identity = keep.tile([P, P], F32, align_bytes=64, name="identity")
+        own_edge = keep.tile([P, EDGES], F32, align_bytes=64, name="own_edge")
+        mix = keep.tile([P, TILES, P], F32, align_bytes=64, name="mix")
+        scratch = keep.tile([P, 1], F32, align_bytes=64, name="scratch")
 
-        def load_scales(dst, scales):
+        x_hbm = x_words.rearrange("g p n -> p g n")
+        rad_hbm = rad.rearrange("e q l -> (e q) l").rearrange("(t p) l -> p t l", p=P)
+        sph_hbm = sph.rearrange("e q j -> (e q) j").rearrange("(t p) j -> p t j", p=P)
+        msg_hbm = msg.rearrange("(k p) n -> p k n", p=P)
+
+        def edge_tile_of(k):
+            return slice(PER_EDGE_TILE * k, PER_EDGE_TILE * (k + 1))
+
+        def bank_of(n):
+            return slice(BANK * n, BANK * (n + 1))
+
+        def load_x(queue, k):
+            queue.dma_start(
+                out=x_w[k][:].bitcast(I32), in_=x_hbm[:, :, X_BYTES * k : X_BYTES * (k + 1)].bitcast(I32)
+            )
+
+        def load_scales(plane, scales):
             for quad in range(4):
                 nc.sync.dma_start(
-                    out=dst[32 * quad : 32 * quad + 4, :, :].bitcast(I32),
+                    out=plane[32 * quad : 32 * quad + 4, :, :].bitcast(I32),
                     in_=scales[:, 4 * quad : 4 * quad + 4, :].rearrange("g r n -> r g n").bitcast(I32),
                 )
 
-        def zero(tile_words):
-            nc.vector.memset(tile_words.bitcast(I32), 0)
-
-        x_hbm = x_words.rearrange("g p n -> p g n")
-        sph_hbm = sph.rearrange("e q j -> (e q) j").rearrange("(t p) j -> p t j", p=P)
-
-        def load_sph(engine, k):
-            with nc.allow_non_contiguous_dma(reason="8-byte rows"):
-                engine.dma_start(out=sph_sb[k][:], in_=sph_hbm[:, TPE * k : TPE * (k + 1), :])
-
-        nc.gpsimd.memset(d_s[:].rearrange("p g n -> p (g n)").bitcast(I32), 0)
-        nc.gpsimd.dma_start(out=x_w[0][:].bitcast(I32), in_=x_hbm[:, :, 0:XC].bitcast(I32))
-        load_sph(nc.gpsimd, 0)
-        make_identity(nc, ident[:])
-        zero(x_s0[:].rearrange("p g n -> p (g n)"))
-        zero(row_d[:])
-        nc.vector.memset(ones[:], 1.0)
-        nc.vector.memset(warm[:], 0.0)
-        load_scales(d_s, d_scales)
-        nc.scalar.dma_start(out=d_w[:].bitcast(I32), in_=d_words.rearrange("g p n -> p g n").bitcast(I32))
-        zero(x_s1[:].rearrange("p g n -> p (g n)"))
-        nc.vector.tensor_reduce(
-            out=mask[:], in_=ident[:].rearrange("p (e q) -> p e q", q=Q), axis=AX.X, op=ALU.add
-        )
-        zero(row_o[:])
-        nc.gpsimd.memset(w_s[:].rearrange("p g n -> p (g n)").bitcast(I32), 0)
-        nc.scalar.dma_start(out=row_d[0:1, :], in_=bias_d.rearrange("(o n) -> o n", o=1))
-        nc.scalar.activation(out=warm[:], in_=warm[:], func=ACT.Silu)
-
-        rad_hbm = rad.rearrange("e q l -> (e q) l").rearrange("(t p) l -> p t l", p=P)
-        msg_hbm = msg.rearrange("(k p) n -> p k n", p=P)
-
-        def load_x(k):
-            nc.sync.dma_start(out=x_w[k][:].bitcast(I32), in_=x_hbm[:, :, XC * k : XC * (k + 1)].bitcast(I32))
+        def load_row(queue, row, vector):
+            queue.dma_start(out=row[0:1, :], in_=vector.rearrange("(o n) -> o n", o=1))
 
         def load_rad(k):
-            nc.sync.dma_start(
-                out=rad_sb[:, TPE * k : TPE * (k + 1), :], in_=rad_hbm[:, TPE * k : TPE * (k + 1), :]
-            )
+            nc.sync.dma_start(out=rad_sb[:, edge_tile_of(k), :], in_=rad_hbm[:, edge_tile_of(k), :])
+
+        def load_sph(queue, k):
+            with nc.allow_non_contiguous_dma(reason="8-byte rows"):
+                queue.dma_start(out=sph_sb[k][:], in_=sph_hbm[:, edge_tile_of(k), :])
+
+        def load_gain():
+            with nc.allow_non_contiguous_dma(reason="8-byte rows"):
+                nc.sync.dma_start(out=gain_sb[:], in_=gain.rearrange("j (m t) -> m j t", t=PACK))
 
         def load_msg(k):
             nc.sync.dma_start(out=msg_sb[:, k, :], in_=msg_hbm[:, k, :])
 
-        load_scales(x_s0, x_scales[:, :, 0 : P * TPE])
+        def zero(engine, rows):
+            engine.memset(rows.bitcast(I32), 0)
+
+        def zero_plane(engine, plane):
+            zero(engine, plane[:].rearrange("p g n -> p (g n)"))
+
+        zero_plane(nc.gpsimd, d_s)
+        load_x(nc.gpsimd, 0)
+        load_sph(nc.gpsimd, 0)
+        make_identity(nc, identity[:])
+        zero_plane(nc.vector, x_s_first)
+        zero(nc.vector, row_d[:])
+        nc.vector.memset(ones[:], 1.0)
+        nc.vector.memset(scratch[:], 0.0)
+        load_scales(d_s, d_scales)
+        nc.scalar.dma_start(out=d_w[:].bitcast(I32), in_=d_words.rearrange("g p n -> p g n").bitcast(I32))
+        zero_plane(nc.vector, x_s_rest)
+        nc.vector.tensor_reduce(
+            out=own_edge[:],
+            in_=identity[:].rearrange("p (e q) -> p e q", q=Q),
+            axis=mybir.AxisListType.X,
+            op=ALU.add,
+        )
+        zero(nc.vector, row_o[:])
+        zero_plane(nc.gpsimd, w_s)
+        load_row(nc.scalar, row_d, bias_d)
+        nc.scalar.activation(out=scratch[:], in_=scratch[:], func=ACT.Silu)
+
+        load_scales(x_s_first, x_scales[:, :, 0:X_COLS])
         load_rad(0)
-        load_scales(x_s1, x_scales[:, :, P * TPE : T])
-        load_x(1)
-        nc.sync.dma_start(out=row_o[0:1, :], in_=bias_o.rearrange("(o n) -> o n", o=1))
+        load_scales(x_s_rest, x_scales[:, :, X_COLS:T])
+        load_x(nc.sync, 1)
+        load_row(nc.sync, row_o, bias_o)
         load_sph(nc.sync, 1)
-        with nc.allow_non_contiguous_dma(reason="small constants"):
-            nc.sync.dma_start(out=gain_sb[:], in_=gain.rearrange("j (m t) -> m j t", t=4))
+        load_gain()
         load_rad(1)
-        load_x(2)
+        load_x(nc.sync, 2)
         load_scales(w_s, w_scales)
         nc.sync.dma_start(out=w_w[:].bitcast(I32), in_=w_words.rearrange("g p n -> p g n").bitcast(I32))
         load_sph(nc.sync, 2)
         load_sph(nc.sync, 3)
         load_rad(2)
-        load_x(3)
+        load_x(nc.sync, 3)
         load_msg(0)
         load_rad(3)
         load_msg(1)
@@ -138,241 +167,237 @@ def tile_triplet_bilinear_messages_f2_kernel(
 
         def warm_up():
             ps = y_pool.tile([P, P], F32, name="y")
-            for i in range(WARM):
+            for i in range(WARM_UP):
                 nc.tensor.matmul(ps[:], ones[:], ones[:], start=True, stop=True)
 
         def spread_bias_d():
             ps = y_pool.tile([P, L], F32, name="y")
             nc.tensor.matmul(ps[:], ones[:], row_d[:], start=True, stop=True)
             nc.scalar.copy(
-                out=bd[:].rearrange("p (t m) -> p t m", t=4), in_=ps[:].rearrange("p (m t) -> p t m", t=4)
+                out=bias_d_all[:].rearrange("p (t m) -> p t m", t=PACK),
+                in_=ps[:].rearrange("p (m t) -> p t m", t=PACK),
             )
 
         def spread_bias_o():
-            for n in range(2):
-                ps = y_pool.tile([P, L], F32, name="y")
-                nc.tensor.matmul(ps[:], ones[:], row_o[:, 512 * n : 512 * (n + 1)], start=True, stop=True)
-                nc.scalar.copy(out=bo[:, 512 * n : 512 * (n + 1)], in_=ps[:])
+            for n in range(HALVES):
+                ps = y_pool.tile([P, BANK], F32, name="y")
+                nc.tensor.matmul(ps[:], ones[:], row_o[:, bank_of(n)], start=True, stop=True)
+                nc.scalar.copy(out=bias_o_all[:, bank_of(n)], in_=ps[:])
 
-        def build_mix(k):
+        def build_first_mix():
+            shape = [P, PER_EDGE_TILE * J, EDGES]
             nc.vector.tensor_tensor(
-                out=mix[:, TPE * k : TPE * (k + 1), :].rearrange("p t (j e) -> p (t j) e", j=J),
-                in0=mask[:].unsqueeze(1).to_broadcast([P, TPE * J, EPT]),
-                in1=sph_sb[k][:]
-                .rearrange("p t j -> p (t j)")
-                .unsqueeze(2)
-                .to_broadcast([P, TPE * J, EPT]),
+                out=mix[:, edge_tile_of(0), :].rearrange("p t (j e) -> p (t j) e", j=J),
+                in0=own_edge[:].unsqueeze(1).to_broadcast(shape),
+                in1=sph_sb[0][:].rearrange("p t j -> p (t j)").unsqueeze(2).to_broadcast(shape),
                 op=ALU.mult,
             )
 
-        def build_mix_piece(k, i):
+        def build_mix(tile):
+            k, i = divmod(tile, PER_EDGE_TILE)
             if i == 0:
-                sph_f[k] = keep.tile([P, TPE * J], F32, align_bytes=64, name="sph_f%d" % k)
-                nc.scalar.copy(out=sph_f[k][:], in_=sph_sb[k][:].rearrange("p t j -> p (t j)"))
+                sph_f32[k] = keep.tile([P, PER_EDGE_TILE * J], F32, align_bytes=64, name="sph_f32_%d" % k)
+                nc.scalar.copy(out=sph_f32[k][:], in_=sph_sb[k][:].rearrange("p t j -> p (t j)"))
             for j in range(J):
                 nc.scalar.activation(
-                    out=mix[:, TPE * k + i, EPT * j : EPT * (j + 1)],
-                    in_=mask[:],
+                    out=mix[:, tile, EDGES * j : EDGES * (j + 1)],
+                    in_=own_edge[:],
                     func=ACT.Copy,
-                    scale=sph_f[k][:, J * i + j : J * i + j + 1],
+                    scale=sph_f32[k][:, J * i + j : J * i + j + 1],
                 )
 
-        sph_f = {}
-        h_of, hb_of, a_of, u_of, v_of = {}, {}, {}, {}, {}
-        z_of, zc_of, zs_of, y_of, ob_of, os_of = {}, {}, {}, {}, {}, {}
+        def scale_msg(k, n):
+            nc.scalar.activation(
+                out=msg_half[k][:, bank_of(n)], in_=msg_sb[:, k, bank_of(n)], func=ACT.Copy, scale=HALF_ROOT
+            )
 
-        def stage1(t):
-            h = h_pool.tile([P, L], F32, name="h")
-            h_of[t] = h
-            scale_plane, col = (x_s0, P * t) if t < TPE else (x_s1, P * (t - TPE))
-            for g in range(G1):
+        h_of, biased_of, act_of, u_of, v_of = {}, {}, {}, {}, {}
+        z_of, codes_of, scales_of, y_of, sum_of = {}, {}, {}, {}, {}
+
+        def project(tile):
+            h_of[tile] = h_pool.tile([P, L], F32, name="h")
+            k, i = divmod(tile, PER_EDGE_TILE)
+            plane, col = (x_s_first, P * tile) if k == 0 else (x_s_rest, P * tile - X_COLS)
+            for g in range(GROUPS):
                 nc.tensor.matmul_mx(
-                    out=h[:],
-                    lhsT=x_w[t // TPE][:, g, 2 * P * (t % TPE) : 2 * P * (t % TPE + 1)].bitcast(FP4X4),
-                    lhsT_scale=scale_plane[:, g, col : col + P],
+                    out=h_of[tile][:],
+                    lhsT=x_w[k][:, g, CODE_BYTES * P * i : CODE_BYTES * P * (i + 1)].bitcast(FP4X4),
+                    lhsT_scale=plane[:, g, col : col + P],
                     rhs=d_w[:, g, :].bitcast(FP4X4),
                     rhs_scale=d_s[:, g, :],
                     start=(g == 0),
-                    stop=(g == G1 - 1),
+                    stop=(g == GROUPS - 1),
                 )
 
-        def add_bias_d(t):
-            hb = work.tile([P, L], F32, align_bytes=64, name="hb")
-            hb_of[t] = hb
+        def add_bias_d(tile):
+            biased_of[tile] = work.tile([P, L], F32, align_bytes=64, name="biased")
             nc.vector.tensor_tensor(
-                out=hb[:].rearrange("p (t m) -> p t m", t=4),
-                in0=h_of[t][:].rearrange("p (m t) -> p t m", t=4),
-                in1=bd[:].rearrange("p (t m) -> p t m", t=4),
+                out=biased_of[tile][:].rearrange("p (t m) -> p t m", t=PACK),
+                in0=h_of[tile][:].rearrange("p (m t) -> p t m", t=PACK),
+                in1=bias_d_all[:].rearrange("p (t m) -> p t m", t=PACK),
                 op=ALU.add,
             )
 
-        def silu_h(t):
-            a = work.tile([P, L], F32, align_bytes=64, name="a")
-            a_of[t] = a
-            nc.scalar.activation(out=a[:], in_=hb_of[t][:], func=ACT.Silu)
+        def silu_h(tile):
+            act_of[tile] = work.tile([P, L], F32, align_bytes=64, name="act")
+            nc.scalar.activation(out=act_of[tile][:], in_=biased_of[tile][:], func=ACT.Silu)
 
-        def times_rad(t):
-            u = work.tile([P, L], F32, align_bytes=64, name="u", bufs=LAG + 3)
-            u_of[t] = u
-            engine = nc.vector if t < 1 else nc.gpsimd
+        def times_rad(engine, tile):
+            u_of[tile] = work.tile([P, L], F32, align_bytes=64, name="u", bufs=LAG + 3)
             engine.tensor_tensor(
-                out=u[:].rearrange("p (t m) -> p t m", t=4),
-                in0=a_of[t][:].rearrange("p (t m) -> p t m", t=4),
-                in1=rad_sb[:, t, :].rearrange("p (m t) -> p t m", t=4),
+                out=u_of[tile][:].rearrange("p (t m) -> p t m", t=PACK),
+                in0=act_of[tile][:].rearrange("p (t m) -> p t m", t=PACK),
+                in1=rad_sb[:, tile, :].rearrange("p (m t) -> p t m", t=PACK),
                 op=ALU.mult,
             )
 
-        def fold(t):
-            v = v_pool.tile([P, 4, P], F32, name="v")
-            v_of[t] = v
-            for i in range(4):
-                nc.tensor.matmul(v[:, i, :], u_of[t][:, P * i : P * (i + 1)], mix[:, t, :], start=True, stop=True)
+        def sum_triplets(tile):
+            v_of[tile] = v_pool.tile([P, PACK, P], F32, name="v")
+            for t in range(PACK):
+                nc.tensor.matmul(
+                    v_of[tile][:, t, :], u_of[tile][:, P * t : P * (t + 1)], mix[:, tile, :], start=True, stop=True
+                )
 
-        def times_gain(t, parts):
-            k, q = divmod(t, TPE)
-            if q == 0:
-                z_of[k] = work.tile([P, J * P * 4], BF16, align_bytes=64, name="z", bufs=2)
-            z4 = z_of[k][:].rearrange("p (j e i) -> p j e i", j=J, i=4)
-            jp = J // parts
-            for i in range(parts):
-                js = slice(jp * i, jp * (i + 1))
+        def times_gain(tile, parts):
+            k, i = divmod(tile, PER_EDGE_TILE)
+            if i == 0:
+                z_of[k] = work.tile([P, J * P * PACK], BF16, align_bytes=64, name="z", bufs=2)
+            z = z_of[k][:].rearrange("p (j e t) -> p j e t", j=J, t=PACK)
+            v = v_of[tile][:].rearrange("p t (j e) -> p j e t", j=J)
+            count = J // parts
+            for part in range(parts):
+                js = slice(count * part, count * (part + 1))
                 nc.vector.tensor_tensor(
-                    out=z4[:, js, EPT * q : EPT * (q + 1), :],
-                    in0=v_of[t][:].rearrange("p i (j e) -> p j e i", j=J)[:, js, :, :],
-                    in1=gain_sb[:, js, :].unsqueeze(2).to_broadcast([P, jp, EPT, 4]),
+                    out=z[:, js, EDGES * i : EDGES * (i + 1), :],
+                    in0=v[:, js, :, :],
+                    in1=gain_sb[:, js, :].unsqueeze(2).to_broadcast([P, count, EDGES, PACK]),
                     op=ALU.mult,
                 )
 
         def quantize(k, parts):
-            zc = work.tile([P, J * P], U32, align_bytes=64, name="zc", bufs=2)
-            zs = work.tile([P, J * P], U8, align_bytes=64, name="zs", bufs=2)
-            zc_of[k], zs_of[k] = zc, zs
-            w = J * P // parts
-            for i in range(parts):
+            codes_of[k] = work.tile([P, J * P], U32, align_bytes=64, name="codes", bufs=2)
+            scales_of[k] = work.tile([P, J * P], U8, align_bytes=64, name="scales", bufs=2)
+            count = J * P // parts
+            for part in range(parts):
+                cols = slice(count * part, count * (part + 1))
                 nc.vector.quantize_mx(
-                    out=zc[:, w * i : w * (i + 1)].bitcast(FP8X4),
-                    scales=zs[:, w * i : w * (i + 1)],
-                    in_=z_of[k][:, 4 * w * i : 4 * w * (i + 1)],
+                    out=codes_of[k][:, cols].bitcast(FP8X4),
+                    scales=scales_of[k][:, cols],
+                    in_=z_of[k][:, PACK * cols.start : PACK * cols.stop],
                 )
 
-        def stage2(k, n, j):
+        def bilinear_pass(k, n, j):
             if j == 0:
-                y_of[k, n] = y_pool.tile([P, 512], F32, name="y")
+                y_of[k, n] = y_pool.tile([P, BANK], F32, name="y")
+            edges = slice(P * j, P * (j + 1))
             nc.tensor.matmul_mx(
                 out=y_of[k, n][:],
-                lhsT=zc_of[k][:, P * j : P * (j + 1)].bitcast(FP8X4),
-                lhsT_scale=zs_of[k][:, P * j : P * (j + 1)],
-                rhs=w_w[:, j, 1024 * n : 1024 * (n + 1)].bitcast(FP4X4),
-                rhs_scale=w_s[:, j, 512 * n : 512 * (n + 1)],
+                lhsT=codes_of[k][:, edges].bitcast(FP8X4),
+                lhsT_scale=scales_of[k][:, edges],
+                rhs=w_w[:, j, CODE_BYTES * BANK * n : CODE_BYTES * BANK * (n + 1)].bitcast(FP4X4),
+                rhs_scale=w_s[:, j, bank_of(n)],
                 start=(j == 0),
                 stop=(j == J - 1),
             )
 
-        def add_bias_o(k, n):
-            ob = work.tile([P, 512], F32, align_bytes=64, name="ob", bufs=4)
-            ob_of[k, n] = ob
-            nc.vector.tensor_tensor(out=ob[:], in0=y_of[k, n][:], in1=bo[:, 512 * n : 512 * (n + 1)], op=ALU.add)
-
-        def silu_y(k, n):
-            so = work.tile([P, 512], F32, align_bytes=64, name="so", bufs=4)
-            os_of[k, n] = so
-            nc.scalar.activation(out=so[:], in_=ob_of[k, n][:], func=ACT.Silu)
+        def silu_of_y(k, n, lo, hi):
+            cols = slice(BANK * n + lo, BANK * n + hi)
+            biased = work.tile([P, hi - lo], F32, align_bytes=64, name="y_biased", bufs=6)
+            act = work.tile([P, hi - lo], F32, align_bytes=64, name="y_act", bufs=6)
+            nc.vector.tensor_tensor(out=biased[:], in0=y_of[k, n][:, lo:hi], in1=bias_o_all[:, cols], op=ALU.add)
+            nc.scalar.activation(out=act[:], in_=biased[:], func=ACT.Silu)
+            return act
 
         def add_msg(k, n):
-            r = work.tile([P, 512], F32, align_bytes=64, name="r")
-            os_of[k, n, "r"] = r
-            nc.gpsimd.tensor_tensor(
-                out=r[:], in0=os_of[k, n][:], in1=msg_sb[:, k, 512 * n : 512 * (n + 1)], op=ALU.add
+            act = silu_of_y(k, n, 0, BANK)
+            sum_of[k, n] = work.tile([P, BANK], F32, align_bytes=64, name="msg_sum")
+            nc.gpsimd.tensor_tensor(out=sum_of[k, n][:], in0=act[:], in1=msg_sb[:, k, bank_of(n)], op=ALU.add)
+
+        def store_scaled(k, n):
+            result = work.tile([P, BANK], F32, align_bytes=64, name="result", bufs=8)
+            nc.scalar.activation(out=result[:], in_=sum_of[k, n][:], func=ACT.Copy, scale=HALF_ROOT)
+            nc.sync.dma_start(out=out[P * k : P * (k + 1), bank_of(n)], in_=result[:])
+
+        def begin_end(k, n):
+            cuts = [(lo, lo + BANK // 2) for lo in (0, BANK // 2)]
+            return [(k, n, lo, hi, silu_of_y(k, n, lo, hi)) for lo, hi in cuts]
+
+        def finish_end(k, n, lo, hi, act):
+            cols = slice(BANK * n + lo, BANK * n + hi)
+            result = work.tile([P, hi - lo], F32, align_bytes=64, name="result", bufs=8)
+            nc.vector.scalar_tensor_tensor(
+                out=result[:], in0=act[:], scalar=HALF_ROOT, in1=msg_half[k][:, cols], op0=ALU.mult, op1=ALU.add
             )
+            nc.sync.dma_start(out=out[P * k : P * (k + 1), cols], in_=result[:])
 
-        def finish(k, n):
-            o = work.tile([P, 512], F32, align_bytes=64, name="o", bufs=6)
-            nc.scalar.activation(out=o[:], in_=os_of[k, n, "r"][:], func=ACT.Copy, scale=HALF)
-            nc.sync.dma_start(out=out[P * k : P * (k + 1), 512 * n : 512 * (n + 1)], in_=o[:])
+        def gain_tiles(step):
+            if step < TILES:
+                return [step - LAG - 1]
+            return [step - LAG - 1, step - LAG] if step == TILES else [step - LAG]
 
-        mc = {k: keep.tile([P, N], F32, align_bytes=64, name="mc%d" % k) for k in (N_ET - 2, N_ET - 1)}
+        def first_pass_step(k):
+            return min(PER_EDGE_TILE * (k + 1) + LAG + 2, TILES + 1)
 
-        def last_output(k, n, lo, hi):
-            cols = slice(512 * n + lo, 512 * n + hi)
-            ob = work.tile([P, hi - lo], F32, align_bytes=64, name="ob", bufs=4)
-            so = work.tile([P, hi - lo], F32, align_bytes=64, name="so", bufs=4)
-            o = work.tile([P, hi - lo], F32, align_bytes=64, name="o", bufs=6)
-            nc.vector.tensor_tensor(out=ob[:], in0=y_of[k, n][:, lo:hi], in1=bo[:, cols], op=ALU.add)
-            nc.scalar.activation(out=so[:], in_=ob[:], func=ACT.Silu)
-            return lambda: (
-                nc.vector.scalar_tensor_tensor(
-                    out=o[:], in0=so[:], scalar=HALF, in1=mc[k][:, cols], op0=ALU.mult, op1=ALU.add
-                ),
-                nc.sync.dma_start(out=out[P * k : P * (k + 1), cols], in_=o[:]),
-            )
-
-        todo = []
-        done1, done2, done3 = [], [], []
-        for step in range(N_TT + LAG):
-            t1, t2 = step, step - LAG
-            if step == 0:
-                warm_up()
-                spread_bias_d()
-            if t1 < N_TT:
-                stage1(t1)
-            if t2 == 0:
+        warm_up()
+        spread_bias_d()
+        warm_up()
+        passes = []
+        done_at = {}
+        for step in range(STEPS):
+            if step < TILES:
+                project(step)
+            if step == LAG:
                 spread_bias_o()
-            if 0 <= t2 < N_TT:
-                fold(t2)
-            finished = []
-            for k, n, j in todo[:2]:
-                if k == N_ET - 2 and n == 1:
-                    break
-                stage2(k, n, j)
-                todo = todo[1:]
-                if j == J - 1:
-                    finished.append((k, n))
+            if step >= LAG:
+                sum_triplets(step - LAG)
+            for k in range(EDGE_TILES - 1):
+                if step == first_pass_step(k):
+                    halves = HALVES if k < EDGE_TILES - 2 else HALVES - 1
+                    passes.extend((k, n, j) for n in range(halves) for j in range(J))
+            take = 2 if step < TILES else 4
+            for k, n, j in passes[:take]:
+                bilinear_pass(k, n, j)
+            done_at[step] = [(k, n) for k, n, j in passes[:take] if j == J - 1]
+            passes = passes[take:]
 
-            if t1 < N_TT:
-                add_bias_d(t1)
-                silu_h(t1)
-                if t1 >= 1:
-                    times_rad(t1)
-                if t1 == 1:
-                    build_mix(0)
-                    times_rad(0)
-            for k, n in done1:
-                add_bias_o(k, n)
-                silu_y(k, n)
+            for k, n in done_at.get(step - 1, []):
                 add_msg(k, n)
-            for k, n in done3:
-                finish(k, n)
-            done3 = done2
-            done2 = done1
-            done1 = finished
-            if 0 <= t2 < N_TT:
-                times_gain(t2, 1 if t2 < N_TT - 1 else 2)
-                if t2 % TPE == TPE - 1:
-                    k = t2 // TPE
-                    quantize(k, 1 if k < N_ET - 1 else 2)
-                    if k < N_ET - 1:
-                        todo.extend((k, n, j) for n in range(2) for j in range(J))
-            if 3 <= step < 3 + N_TT - TPE:
-                build_mix_piece(*divmod(step - 3 + TPE, TPE))
-            if step == 11:
-                cols = slice(512, 1024)
-                nc.scalar.activation(
-                    out=mc[N_ET - 2][:, cols], in_=msg_sb[:, N_ET - 2, cols], func=ACT.Copy, scale=HALF
-                )
-            if step in (12, 13):
-                cols = slice(512 * (step - 12), 512 * (step - 11))
-                nc.scalar.activation(
-                    out=mc[N_ET - 1][:, cols], in_=msg_sb[:, N_ET - 1, cols], func=ACT.Copy, scale=HALF
-                )
-        for k, n in done3:
-            finish(k, n)
-        waiting = []
-        for k, n in ((N_ET - 2, 1), (N_ET - 1, 0), (N_ET - 1, 1)):
+            tiles = [tile for tile in gain_tiles(step) if tile >= 0]
+            for tile in tiles:
+                times_gain(tile, 1 if tile < TILES - 1 else 2)
+            if step < TILES:
+                add_bias_d(step)
+                silu_h(step)
+            if step == 1:
+                build_first_mix()
+                times_rad(nc.vector, 0)
+            if 1 <= step < TILES:
+                times_rad(nc.gpsimd, step)
+            for tile in tiles:
+                k, i = divmod(tile, PER_EDGE_TILE)
+                if i == PER_EDGE_TILE - 1:
+                    quantize(k, 1 if k < EDGE_TILES - 1 else 2)
+            for k, n in done_at.get(step - 3, []):
+                store_scaled(k, n)
+
+            if PER_EDGE_TILE <= step + 1 < TILES:
+                build_mix(step + 1)
+            if 11 <= step <= 13:
+                scale_msg(*[(EDGE_TILES - 2, 1), (EDGE_TILES - 1, 0), (EDGE_TILES - 1, 1)][step - 11])
+
+        banks = [(EDGE_TILES - 2, 1), (EDGE_TILES - 1, 0), (EDGE_TILES - 1, 1)]
+        for j in range(J):
+            bilinear_pass(*banks[0], j)
+        begun = begin_end(*banks[0])
+        for step in range(STEPS - 3, STEPS):
+            for k, n in done_at[step]:
+                store_scaled(k, n)
+        for part in begun:
+            finish_end(*part)
+        begun = []
+        for k, n in banks[1:]:
             for j in range(J):
-                stage2(k, n, j)
-            halves = [last_output(k, n, lo, lo + 256) for lo in (0, 256)]
-            for last in waiting:
-                last()
-            waiting = halves
-        for last in waiting:
-            last()
+                bilinear_pass(k, n, j)
+            begun.extend(begin_end(k, n))
+        for part in begun:
+            finish_end(*part)

import math
from contextlib import ExitStack

import concourse.mybir as mybir
from concourse.masks import make_identity

E, Q, J, L, K, N = 512, 4, 4, 512, 1024, 1024
T = E * Q

F32 = mybir.dt.float32
BF16 = mybir.dt.bfloat16
U32 = mybir.dt.uint32
I32 = mybir.dt.int32
U8 = mybir.dt.uint8
FP8X4 = mybir.dt.float8_e4m3fn_x4
FP4X4 = mybir.dt.float4_e2m1fn_x4
ACT = mybir.ActivationFunctionType
ALU = mybir.AluOpType

FLOPS = 2 * T * K * L + 2 * E * (J * L) * N

P = 128
PACK = 4
GROUPS = K // (P * PACK)
BANK = 512
TILES = T // P
EDGE_TILES = E // P
PER_EDGE_TILE = TILES // EDGE_TILES
EDGES = P // Q
HALVES = N // BANK
CODE_BYTES = 2
X_BYTES = CODE_BYTES * P * PER_EDGE_TILE
X_COLS = P * PER_EDGE_TILE
HALF_ROOT = math.sqrt(0.5)

LAG = 4
STEPS = TILES + LAG
WARM_UP = 10


def tile_triplet_bilinear_messages_f2_kernel(
    tc, x_words, x_scales, d_words, d_scales, bias_d, rad, sph, gain, w_words, w_scales, bias_o, msg, out
):
    nc = tc.nc
    with ExitStack() as ctx:
        keep = ctx.enter_context(tc.tile_pool(name="keep", bufs=1))
        work = ctx.enter_context(tc.tile_pool(name="work", bufs=3))
        h_pool = ctx.enter_context(tc.psum_pool(name="h_pool", bufs=3))
        v_pool = ctx.enter_context(tc.psum_pool(name="v_pool", bufs=3))
        y_pool = ctx.enter_context(tc.psum_pool(name="y_pool", bufs=2))
        ctx.enter_context(tc.manual_schedule())

        x_w = [keep.tile([P, GROUPS, X_BYTES], U8, align_bytes=64, name="x_w%d" % k) for k in range(EDGE_TILES)]
        x_s_first = keep.tile([P, GROUPS, X_COLS], U8, align_bytes=64, name="x_s_first")
        x_s_rest = keep.tile([P, GROUPS, T - X_COLS], U8, align_bytes=64, name="x_s_rest")
        d_w = keep.tile([P, GROUPS, CODE_BYTES * L], U8, align_bytes=64, name="d_w")
        d_s = keep.tile([P, GROUPS, L], U8, align_bytes=64, name="d_s")
        w_w = keep.tile([P, J, CODE_BYTES * N], U8, align_bytes=64, name="w_w")
        w_s = keep.tile([P, J, N], U8, align_bytes=64, name="w_s")

        rad_sb = keep.tile([P, TILES, L], BF16, align_bytes=64, name="rad_sb")
        sph_sb = [keep.tile([P, PER_EDGE_TILE, J], BF16, align_bytes=64, name="sph_sb%d" % k) for k in range(EDGE_TILES)]
        sph_f32 = {}
        gain_sb = keep.tile([P, J, PACK], BF16, align_bytes=64, name="gain_sb")
        msg_sb = keep.tile([P, EDGE_TILES, N], BF16, align_bytes=64, name="msg_sb")
        msg_half = {
            k: keep.tile([P, N], F32, align_bytes=64, name="msg_half%d" % k) for k in (EDGE_TILES - 2, EDGE_TILES - 1)
        }
        row_d = keep.tile([P, L], BF16, align_bytes=64, name="row_d")
        row_o = keep.tile([P, N], BF16, align_bytes=64, name="row_o")
        ones = keep.tile([P, P], BF16, align_bytes=64, name="ones")
        bias_d_all = keep.tile([P, L], F32, align_bytes=64, name="bias_d_all")
        bias_o_all = keep.tile([P, N], F32, align_bytes=64, name="bias_o_all")
        identity = keep.tile([P, P], F32, align_bytes=64, name="identity")
        own_edge = keep.tile([P, EDGES], F32, align_bytes=64, name="own_edge")
        mix = keep.tile([P, TILES, P], F32, align_bytes=64, name="mix")
        scratch = keep.tile([P, 1], F32, align_bytes=64, name="scratch")

        x_hbm = x_words.rearrange("g p n -> p g n")
        rad_hbm = rad.rearrange("e q l -> (e q) l").rearrange("(t p) l -> p t l", p=P)
        sph_hbm = sph.rearrange("e q j -> (e q) j").rearrange("(t p) j -> p t j", p=P)
        msg_hbm = msg.rearrange("(k p) n -> p k n", p=P)

        def edge_tile_of(k):
            return slice(PER_EDGE_TILE * k, PER_EDGE_TILE * (k + 1))

        def bank_of(n):
            return slice(BANK * n, BANK * (n + 1))

        def load_x(queue, k):
            queue.dma_start(
                out=x_w[k][:].bitcast(I32), in_=x_hbm[:, :, X_BYTES * k : X_BYTES * (k + 1)].bitcast(I32)
            )

        def load_scales(plane, scales):
            for quad in range(4):
                nc.sync.dma_start(
                    out=plane[32 * quad : 32 * quad + 4, :, :].bitcast(I32),
                    in_=scales[:, 4 * quad : 4 * quad + 4, :].rearrange("g r n -> r g n").bitcast(I32),
                )

        def load_row(queue, row, vector):
            queue.dma_start(out=row[0:1, :], in_=vector.rearrange("(o n) -> o n", o=1))

        def load_rad(k):
            nc.sync.dma_start(out=rad_sb[:, edge_tile_of(k), :], in_=rad_hbm[:, edge_tile_of(k), :])

        def load_sph(queue, k):
            with nc.allow_non_contiguous_dma(reason="8-byte rows"):
                queue.dma_start(out=sph_sb[k][:], in_=sph_hbm[:, edge_tile_of(k), :])

        def load_gain():
            with nc.allow_non_contiguous_dma(reason="8-byte rows"):
                nc.sync.dma_start(out=gain_sb[:], in_=gain.rearrange("j (m t) -> m j t", t=PACK))

        def load_msg(k):
            nc.sync.dma_start(out=msg_sb[:, k, :], in_=msg_hbm[:, k, :])

        def zero(engine, rows):
            engine.memset(rows.bitcast(I32), 0)

        def zero_plane(engine, plane):
            zero(engine, plane[:].rearrange("p g n -> p (g n)"))

        zero_plane(nc.gpsimd, d_s)
        load_x(nc.gpsimd, 0)
        load_sph(nc.gpsimd, 0)
        make_identity(nc, identity[:])
        zero_plane(nc.vector, x_s_first)
        zero(nc.vector, row_d[:])
        nc.vector.memset(ones[:], 1.0)
        nc.vector.memset(scratch[:], 0.0)
        load_scales(d_s, d_scales)
        nc.scalar.dma_start(out=d_w[:].bitcast(I32), in_=d_words.rearrange("g p n -> p g n").bitcast(I32))
        zero_plane(nc.vector, x_s_rest)
        nc.vector.tensor_reduce(
            out=own_edge[:],
            in_=identity[:].rearrange("p (e q) -> p e q", q=Q),
            axis=mybir.AxisListType.X,
            op=ALU.add,
        )
        zero(nc.vector, row_o[:])
        zero_plane(nc.gpsimd, w_s)
        load_row(nc.scalar, row_d, bias_d)
        nc.scalar.activation(out=scratch[:], in_=scratch[:], func=ACT.Silu)

        load_scales(x_s_first, x_scales[:, :, 0:X_COLS])
        load_rad(0)
        load_scales(x_s_rest, x_scales[:, :, X_COLS:T])
        load_x(nc.sync, 1)
        load_row(nc.sync, row_o, bias_o)
        load_sph(nc.sync, 1)
        load_gain()
        load_rad(1)
        load_x(nc.sync, 2)
        load_scales(w_s, w_scales)
        nc.sync.dma_start(out=w_w[:].bitcast(I32), in_=w_words.rearrange("g p n -> p g n").bitcast(I32))
        load_sph(nc.sync, 2)
        load_sph(nc.sync, 3)
        load_rad(2)
        load_x(nc.sync, 3)
        load_msg(0)
        load_rad(3)
        load_msg(1)
        load_msg(2)
        load_msg(3)

        def warm_up():
            ps = y_pool.tile([P, P], F32, name="y")
            for i in range(WARM_UP):
                nc.tensor.matmul(ps[:], ones[:], ones[:], start=True, stop=True)

        def spread_bias_d():
            ps = y_pool.tile([P, L], F32, name="y")
            nc.tensor.matmul(ps[:], ones[:], row_d[:], start=True, stop=True)
            nc.scalar.copy(
                out=bias_d_all[:].rearrange("p (t m) -> p t m", t=PACK),
                in_=ps[:].rearrange("p (m t) -> p t m", t=PACK),
            )

        def spread_bias_o():
            for n in range(HALVES):
                ps = y_pool.tile([P, BANK], F32, name="y")
                nc.tensor.matmul(ps[:], ones[:], row_o[:, bank_of(n)], start=True, stop=True)
                nc.scalar.copy(out=bias_o_all[:, bank_of(n)], in_=ps[:])

        def build_first_mix():
            shape = [P, PER_EDGE_TILE * J, EDGES]
            nc.vector.tensor_tensor(
                out=mix[:, edge_tile_of(0), :].rearrange("p t (j e) -> p (t j) e", j=J),
                in0=own_edge[:].unsqueeze(1).to_broadcast(shape),
                in1=sph_sb[0][:].rearrange("p t j -> p (t j)").unsqueeze(2).to_broadcast(shape),
                op=ALU.mult,
            )

        def build_mix(tile):
            k, i = divmod(tile, PER_EDGE_TILE)
            if i == 0:
                sph_f32[k] = keep.tile([P, PER_EDGE_TILE * J], F32, align_bytes=64, name="sph_f32_%d" % k)
                nc.scalar.copy(out=sph_f32[k][:], in_=sph_sb[k][:].rearrange("p t j -> p (t j)"))
            for j in range(J):
                nc.scalar.activation(
                    out=mix[:, tile, EDGES * j : EDGES * (j + 1)],
                    in_=own_edge[:],
                    func=ACT.Copy,
                    scale=sph_f32[k][:, J * i + j : J * i + j + 1],
                )

        def scale_msg(k, n):
            nc.scalar.activation(
                out=msg_half[k][:, bank_of(n)], in_=msg_sb[:, k, bank_of(n)], func=ACT.Copy, scale=HALF_ROOT
            )

        h_of, biased_of, act_of, u_of, v_of = {}, {}, {}, {}, {}
        z_of, codes_of, scales_of, y_of, sum_of = {}, {}, {}, {}, {}

        def project(tile):
            h_of[tile] = h_pool.tile([P, L], F32, name="h")
            k, i = divmod(tile, PER_EDGE_TILE)
            plane, col = (x_s_first, P * tile) if k == 0 else (x_s_rest, P * tile - X_COLS)
            for g in range(GROUPS):
                nc.tensor.matmul_mx(
                    out=h_of[tile][:],
                    lhsT=x_w[k][:, g, CODE_BYTES * P * i : CODE_BYTES * P * (i + 1)].bitcast(FP4X4),
                    lhsT_scale=plane[:, g, col : col + P],
                    rhs=d_w[:, g, :].bitcast(FP4X4),
                    rhs_scale=d_s[:, g, :],
                    start=(g == 0),
                    stop=(g == GROUPS - 1),
                )

        def add_bias_d(tile):
            biased_of[tile] = work.tile([P, L], F32, align_bytes=64, name="biased")
            nc.vector.tensor_tensor(
                out=biased_of[tile][:].rearrange("p (t m) -> p t m", t=PACK),
                in0=h_of[tile][:].rearrange("p (m t) -> p t m", t=PACK),
                in1=bias_d_all[:].rearrange("p (t m) -> p t m", t=PACK),
                op=ALU.add,
            )

        def silu_h(tile):
            act_of[tile] = work.tile([P, L], F32, align_bytes=64, name="act")
            nc.scalar.activation(out=act_of[tile][:], in_=biased_of[tile][:], func=ACT.Silu)

        def times_rad(engine, tile):
            u_of[tile] = work.tile([P, L], F32, align_bytes=64, name="u", bufs=LAG + 3)
            engine.tensor_tensor(
                out=u_of[tile][:].rearrange("p (t m) -> p t m", t=PACK),
                in0=act_of[tile][:].rearrange("p (t m) -> p t m", t=PACK),
                in1=rad_sb[:, tile, :].rearrange("p (m t) -> p t m", t=PACK),
                op=ALU.mult,
            )

        def sum_triplets(tile):
            v_of[tile] = v_pool.tile([P, PACK, P], F32, name="v")
            for t in range(PACK):
                nc.tensor.matmul(
                    v_of[tile][:, t, :], u_of[tile][:, P * t : P * (t + 1)], mix[:, tile, :], start=True, stop=True
                )

        def times_gain(tile, parts):
            k, i = divmod(tile, PER_EDGE_TILE)
            if i == 0:
                z_of[k] = work.tile([P, J * P * PACK], BF16, align_bytes=64, name="z", bufs=2)
            z = z_of[k][:].rearrange("p (j e t) -> p j e t", j=J, t=PACK)
            v = v_of[tile][:].rearrange("p t (j e) -> p j e t", j=J)
            count = J // parts
            for part in range(parts):
                js = slice(count * part, count * (part + 1))
                nc.vector.tensor_tensor(
                    out=z[:, js, EDGES * i : EDGES * (i + 1), :],
                    in0=v[:, js, :, :],
                    in1=gain_sb[:, js, :].unsqueeze(2).to_broadcast([P, count, EDGES, PACK]),
                    op=ALU.mult,
                )

        def quantize(k, parts):
            codes_of[k] = work.tile([P, J * P], U32, align_bytes=64, name="codes", bufs=2)
            scales_of[k] = work.tile([P, J * P], U8, align_bytes=64, name="scales", bufs=2)
            count = J * P // parts
            for part in range(parts):
                cols = slice(count * part, count * (part + 1))
                nc.vector.quantize_mx(
                    out=codes_of[k][:, cols].bitcast(FP8X4),
                    scales=scales_of[k][:, cols],
                    in_=z_of[k][:, PACK * cols.start : PACK * cols.stop],
                )

        def bilinear_pass(k, n, j):
            if j == 0:
                y_of[k, n] = y_pool.tile([P, BANK], F32, name="y")
            edges = slice(P * j, P * (j + 1))
            nc.tensor.matmul_mx(
                out=y_of[k, n][:],
                lhsT=codes_of[k][:, edges].bitcast(FP8X4),
                lhsT_scale=scales_of[k][:, edges],
                rhs=w_w[:, j, CODE_BYTES * BANK * n : CODE_BYTES * BANK * (n + 1)].bitcast(FP4X4),
                rhs_scale=w_s[:, j, bank_of(n)],
                start=(j == 0),
                stop=(j == J - 1),
            )

        def silu_of_y(k, n, lo, hi):
            cols = slice(BANK * n + lo, BANK * n + hi)
            biased = work.tile([P, hi - lo], F32, align_bytes=64, name="y_biased", bufs=6)
            act = work.tile([P, hi - lo], F32, align_bytes=64, name="y_act", bufs=6)
            nc.vector.tensor_tensor(out=biased[:], in0=y_of[k, n][:, lo:hi], in1=bias_o_all[:, cols], op=ALU.add)
            nc.scalar.activation(out=act[:], in_=biased[:], func=ACT.Silu)
            return act

        def add_msg(k, n):
            act = silu_of_y(k, n, 0, BANK)
            sum_of[k, n] = work.tile([P, BANK], F32, align_bytes=64, name="msg_sum")
            nc.gpsimd.tensor_tensor(out=sum_of[k, n][:], in0=act[:], in1=msg_sb[:, k, bank_of(n)], op=ALU.add)

        def store_scaled(k, n):
            result = work.tile([P, BANK], F32, align_bytes=64, name="result", bufs=8)
            nc.scalar.activation(out=result[:], in_=sum_of[k, n][:], func=ACT.Copy, scale=HALF_ROOT)
            nc.sync.dma_start(out=out[P * k : P * (k + 1), bank_of(n)], in_=result[:])

        def begin_end(k, n):
            cuts = [(lo, lo + BANK // 2) for lo in (0, BANK // 2)]
            return [(k, n, lo, hi, silu_of_y(k, n, lo, hi)) for lo, hi in cuts]

        def finish_end(k, n, lo, hi, act):
            cols = slice(BANK * n + lo, BANK * n + hi)
            result = work.tile([P, hi - lo], F32, align_bytes=64, name="result", bufs=8)
            nc.vector.scalar_tensor_tensor(
                out=result[:], in0=act[:], scalar=HALF_ROOT, in1=msg_half[k][:, cols], op0=ALU.mult, op1=ALU.add
            )
            nc.sync.dma_start(out=out[P * k : P * (k + 1), cols], in_=result[:])

        def gain_tiles(step):
            if step < TILES:
                return [step - LAG - 1]
            return [step - LAG - 1, step - LAG] if step == TILES else [step - LAG]

        def first_pass_step(k):
            return min(PER_EDGE_TILE * (k + 1) + LAG + 2, TILES + 1)

        warm_up()
        spread_bias_d()
        warm_up()
        passes = []
        done_at = {}
        for step in range(STEPS):
            if step < TILES:
                project(step)
            if step == LAG:
                spread_bias_o()
            if step >= LAG:
                sum_triplets(step - LAG)
            for k in range(EDGE_TILES - 1):
                if step == first_pass_step(k):
                    halves = HALVES if k < EDGE_TILES - 2 else HALVES - 1
                    passes.extend((k, n, j) for n in range(halves) for j in range(J))
            take = 2 if step < TILES else 4
            for k, n, j in passes[:take]:
                bilinear_pass(k, n, j)
            done_at[step] = [(k, n) for k, n, j in passes[:take] if j == J - 1]
            passes = passes[take:]

            for k, n in done_at.get(step - 1, []):
                add_msg(k, n)
            tiles = [tile for tile in gain_tiles(step) if tile >= 0]
            for tile in tiles:
                times_gain(tile, 1 if tile < TILES - 1 else 2)
            if step < TILES:
                add_bias_d(step)
                silu_h(step)
            if step == 1:
                build_first_mix()
                times_rad(nc.vector, 0)
            if 1 <= step < TILES:
                times_rad(nc.gpsimd, step)
            for tile in tiles:
                k, i = divmod(tile, PER_EDGE_TILE)
                if i == PER_EDGE_TILE - 1:
                    quantize(k, 1 if k < EDGE_TILES - 1 else 2)
            for k, n in done_at.get(step - 3, []):
                store_scaled(k, n)

            if PER_EDGE_TILE <= step + 1 < TILES:
                build_mix(step + 1)
            if 11 <= step <= 13:
                scale_msg(*[(EDGE_TILES - 2, 1), (EDGE_TILES - 1, 0), (EDGE_TILES - 1, 1)][step - 11])

        banks = [(EDGE_TILES - 2, 1), (EDGE_TILES - 1, 0), (EDGE_TILES - 1, 1)]
        for j in range(J):
            bilinear_pass(*banks[0], j)
        begun = begin_end(*banks[0])
        for step in range(STEPS - 3, STEPS):
            for k, n in done_at[step]:
                store_scaled(k, n)
        for part in begun:
            finish_end(*part)
        begun = []
        for k, n in banks[1:]:
            for j in range(J):
                bilinear_pass(k, n, j)
            begun.extend(begin_end(k, n))
        for part in begun:
            finish_end(*part)
